import numpy as np, ml_dtypes
CORES = [24,25,26,27,28,29,30,31]
N = 8
BF = ml_dtypes.bfloat16
B, W, CAP, RO = 2048, 6144, 48, 3
L = N * CAP
def parts(rng):
    share = rng.choice(np.array([0.1, 0.2, 0.4, 0.6]), (N, 8, 1, B))
    v = np.where(rng.random((N, 8, 16, B)) < share, -rng.integers(1, 256, (N, 8, 16, B)), rng.integers(0, 256, (N, 8, 16, B)))
    a = rng.integers(0, 256, (N, 8, 16, W)) * (rng.random((N, 8, 16, W)) < rng.choice(np.array([0.3, 0.6, 0.9]), (N, 8, 1, W))); a[..., W - 1] = 0
    u = rng.integers(0, W - 1, (N, 8, 16, B))
    u = np.where(rng.random(u.shape) < rng.choice(np.array([0.0, 0.0, 0.1, 0.1, 0.4, 0.96]), (N, 8, 1, B)), W - 1, u)
    to = np.where(rng.random((N, 8, W)) < rng.choice(np.array([0.0, 0.1, 0.25]), (N, 8, 1)), rng.integers(0, N, (N, 8, 1)), rng.integers(0, N, (N, 8, W)))
    pay = to * B + rng.integers(0, B, (N, 8, W))
    wk = np.where(rng.random((N, 8, L)) < 0.04, B, rng.integers(0, B, (N, 8, L)))
    return v, a, u, pay, wk
def pack(v, a, u, pay, wk):
    return {"vp": np.ascontiguousarray(v.reshape(N, 128, B)).astype(np.float32).astype(BF), "am": np.ascontiguousarray(a.reshape(N, 128, W)).astype(np.float32).astype(BF),
            "qu": np.ascontiguousarray(u.reshape(N, 128, B)).astype(np.int32), "pay": np.ascontiguousarray(pay).astype(np.int32), "wk": np.ascontiguousarray(wk).astype(np.int32)}
def setup_inputs(rng):
    return pack(*parts(rng))
def plant(rng, v, a, u, pay, wk, q, g, to):
    m = len(to); lanes = rng.permutation(L)[:m]; banks = rng.permutation(B)[:m]; lines = rng.permutation(W - 1)[:m]
    row = rng.integers(0, 16, m); j = rng.integers(0, 16, m)
    u[q, g][:, banks] = W - 1; u[q, g][row, banks] = lines
    v[q, g][j, banks] = -rng.integers(1, 256, m); a[q, g][j, lines] = 255
    order = np.argsort(lanes); pay[q, g][lines[order]] = to
    wk[q, g] = B; wk[q, g][lanes] = banks
def setup_inputs_room(rng):
    v, a, u, pay, wk = parts(rng)
    for q in range(N):
        for g in range(8):
            cnt = [CAP, CAP + 1, CAP - 1, 0, 1, 0, 2, CAP // 2][:N]
            if (q + g) % 4 == 3: cnt = [L] + [0] * (N - 1)
            to = np.concatenate([np.full(n, (q + 1 + g + j) % N, np.int64) for j, n in enumerate(cnt)])
            plant(rng, v, a, u, pay, wk, q, g, rng.permutation(to) * B + rng.integers(0, B, len(to)))
    return pack(v, a, u, pay, wk)
def setup_inputs_ties(rng):
    v, a, u, pay, wk = parts(rng)
    v[:, ::2] = rng.integers(-3, 3, (N, 4, 16, B)); a[:, ::2] = rng.integers(0, 4, (N, 4, 16, W))
    v[:, 1::2] = rng.integers(-3, 2, (N, 4, 16, B)) * 85; a[:, 1::2] = rng.integers(0, 4, (N, 4, 16, W)) * 85
    a = a * (rng.random((N, 8, 1, W)) < 0.6); a[..., W - 1] = 0
    u[:, :, 15] = np.where(rng.random((N, 8, B)) < 0.4, W - 1, u[:, :, 15])
    return pack(v, a, u, pay, wk)
def setup_inputs_alike(rng):
    v, a, u, pay, wk = parts(rng)
    wk[:, 0] = rng.choice(np.array([0, B - 1, 5, B // 2]), (N, L))
    u[:, 2] = rng.choice(np.array([0, W - 2, 7, W // 2, W - 1]), (N, 16, B))
    pay[:, 4] = rng.integers(0, N, (N, W)) * B + rng.choice(np.array([0, B - 1]), (N, W))
    u[:, 6] = np.repeat(u[:, 6, :1], 16, axis=1)
    wk[:, 1::2, L - 1] = wk[:, 1::2, 0]
    return pack(v, a, u, pay, wk)
def setup_inputs_dry(rng):
    v, a, u, pay, wk = parts(rng); o = rng.permutation(8)
    wk[:, o[0]] = B; a[:, o[1]] = 0; u[:, o[2]] = W - 1; v[:, o[3]] = np.abs(v[:, o[3]])
    v[:, o[4]] = -255; a[:, o[4]] = 255; a[..., W - 1] = 0
    wk[rng.integers(0, N), o[5]] = B
    h = int(o[6]); wk[:, h] = B
    for q in range(N):
        b = int(rng.integers(1, B)); n, m = [int(i) for i in rng.permutation(W - 1)[:2]]
        wk[q, h, int(rng.integers(0, L))] = b
        v[q, h, :, b] = -rng.integers(1, 256, 16); u[q, h, :, b] = n; a[q, h, :, n] = 0; pay[q, h, n] = (q + 1) % N * B
        v[q, h, :, 0] = -rng.integers(1, 256, 16); u[q, h, :, 0] = m; a[q, h, :, m] = 255; pay[q, h, m] = rng.integers(0, N) * B + rng.integers(1, B)
    return pack(v, a, u, pay, wk)
def setup_inputs_spread(rng):
    v, a, u, pay, wk = parts(rng)
    v = (np.exp2(8 * rng.random((N, 8, 1, B))) * rng.random((N, 8, 16, B))).astype(np.int64) * np.where(rng.random((N, 8, 16, B)) < 0.4, -1, 1)
    a = (np.exp2(8 * rng.random((N, 8, 1, W))) * rng.random((N, 8, 16, W))).astype(np.int64); a[..., W - 1] = 0
    u = np.where(u == W - 1, u, ((W - 1) * rng.random(u.shape) ** 2).astype(np.int64))
    pay = pay // B * B + (B * rng.random(pay.shape) ** 2).astype(np.int64)
    wk = np.where(wk == B, B, (B * rng.random(wk.shape) ** 2).astype(np.int64))
    return pack(v, a, u, pay, wk)
def check_inputs(d):
    bad = []
    for k, lo, hi in (("vp", -255, 255), ("am", 0, 255)):
        x = np.asarray(d[k]).astype(np.float32)
        if not np.all((x >= lo) & (x <= hi)): bad.append("range of " + k)
        elif not np.all(x == np.rint(x)): bad.append("whole numbers in " + k)
    if not np.all(np.asarray(d["am"]).astype(np.float32)[..., W - 1] == 0): bad.append("zeros in the last column of am")
    for k, hi in (("qu", W - 1), ("pay", N * B - 1), ("wk", B)):
        if np.min(d[k]) < 0 or np.max(d[k]) > hi: bad.append("range of " + k)
    return bad
def reference(vp, am, qu, pay, wk):
    v = vp.astype(np.float32).astype(np.int64).reshape(N, 8, 16, B); a = am.astype(np.float32).astype(np.int64).reshape(N, 8, 16, W)
    u = qu.astype(np.int64).reshape(N, 8, 16, B); payee = pay.astype(np.int64)
    w = wk.astype(np.int64); c = np.zeros((N, 8, 16, L), np.int64)
    for rnd in range(RO):
        w2 = np.full((N, 8, L), B, np.int64); c2 = np.zeros((N, 8, 16, L), np.int64)
        for q in range(N):
            for g in range(8):
                vv, aa, uu = v[q, g], a[q, g], u[q, g]
                lane = np.nonzero(w[q, g] < B)[0]
                lane = lane[np.sort(np.unique(w[q, g][lane], return_index=True)[1])]
                b = w[q, g][lane]
                x = np.maximum(vv[:, b] - c[q, g][:, lane], -255); vv[:, b] = x
                keep = np.any(x < 0, axis=0); b, x = b[keep], x[:, keep]
                n = uu[:, b]
                score = np.sum(x[:, None, :] + aa[:, n] >= 0, axis=0)
                best = 15 - np.argmax(score[::-1], axis=0)
                p = n[best, np.arange(len(b))]
                keep = p != W - 1; b, x, best, p = b[keep], x[:, keep], best[keep], p[keep]
                keep = np.sort(np.unique(p, return_index=True)[1]); b, x, best, p = b[keep], x[:, keep], best[keep], p[keep]
                t = np.minimum(aa[:, p], np.maximum(-x, 0))
                vv[:, b] = x + t; aa[:, p] = aa[:, p] - t; uu[best, b] = W - 1
                to = payee[q, g][p]
                for r in range(N):
                    k = np.nonzero(to // B == r)[0][:CAP]; s = q * CAP + np.arange(len(k))
                    w2[r, g][s] = to[k] % B; c2[r, g][:, s] = t[:, k]
        w, c = w2, c2
    return {"yv": v.reshape(N, 128, B).astype(np.float32).astype(BF), "yw": w.astype(np.float32), "yc": c.reshape(N, 128, L).astype(np.float32).astype(BF)}

@@ -1,0 +1,437 @@
+from concourse.bass import DstId, RemoteDMATransfer
+from concourse.mybir import AluOpType, ActivationFunctionType
+
+A = AluOpType
+F = ActivationFunctionType
+NR, B, W, CAP, RO = 8, 2048, 6144, 48, 3
+L = NR * CAP
+VW = 2560
+AW = 6544
+PITCH = 400
+SW = 3600
+BIG = 8388608.0
+SC = 131072.0
+NA = 4
+K_SCORE, K_PAIRS, K_VAL = 2, 3, 5
+
+SCRATCH = {
+    "vw": ("sbuf", [128, VW], "bfloat16"), "qw": ("sbuf", [128, VW], "int32"), "aw": ("sbuf", [128, AW], "bfloat16"),
+    "pw": ("sbuf", [128, W], "int32"), "hw": ("sbuf", [128, W], "float32"), "wn": ("sbuf", [128, 32], "float32"),
+    "cc": ("sbuf", [128, 24, 256], "bfloat16"), "gg": ("sbuf", [128, L * 16], "bfloat16"),
+    "vr": ("sbuf", [128, L * 16], "bfloat16"), "ee": ("sbuf", [128, 24, L], "bfloat16"),
+    "lm": ("sbuf", [128, 16, 128], "bfloat16"), "tm": ("sbuf", [128, 16, 128], "bfloat16"),
+    "rm": ("sbuf", [128, 2048], "bfloat16"), "ir": ("sbuf", [128, 2048], "bfloat16"),
+    "bo": ("sbuf", [128, 128], "bfloat16"), "bp": ("sbuf", [128, 128], "bfloat16"), "idb": ("sbuf", [128, 128], "bfloat16"),
+    "zb": ("sbuf", [128, L], "bfloat16"), "dsf": ("sbuf", [128, 4, 128], "float32"), "dsb": ("sbuf", [128, 4, 128], "bfloat16"),
+    "pi": ("sbuf", [128, 4], "int32"), "io128": ("sbuf", [128, 128], "bfloat16"), "iog": ("sbuf", [128, 128], "bfloat16"),
+    "io16": ("sbuf", [128, 16], "bfloat16"), "trv": ("sbuf", [128, 24], "float32"), "wc": ("sbuf", [128, 48], "float32"),
+    "col": ("sbuf", [128, 16], "float32"), "wkz": ("sbuf", [128, L], "int32"), "w16": ("sbuf", [128, L], "float16"),
+    "land1": ("sbuf", [128, L], "float32"), "land2": ("sbuf", [128, L], "float32"), "land3": ("sbuf", [128, L], "float32"),
+    "sw0": ("sbuf", [128, SW], "float32"), "sw1": ("sbuf", [128, SW], "float32"), "sw2": ("sbuf", [128, SW], "float32"),
+    "tt": ("sbuf", [128, L], "float32"), "tqi": ("sbuf", [128, 24], "int32"), "tq": ("sbuf", [128, 24], "float16"),
+    "bl": ("sbuf", [128, 24], "uint16"), "bf": ("sbuf", [128, 24], "float32"), "b16": ("sbuf", [128, L], "float16"),
+    "yy": ("sbuf", [128, L], "float32"), "li": ("sbuf", [128, L], "int32"), "ci": ("sbuf", [128, L], "int32"),
+    "cb": ("sbuf", [128, L], "bfloat16"), "q16": ("sbuf", [128, L], "uint16"), "qf": ("sbuf", [128, L], "float32"),
+    "qt": ("sbuf", [128, 12, 32], "float32"), "k1s": ("sbuf", [128, 24, 16], "float32"), "kk": ("sbuf", [128, 24, 16], "float32"),
+    "t8": ("sbuf", [128, 24, 8], "float32"), "t4": ("sbuf", [128, 24, 4], "float32"), "t2": ("sbuf", [128, 24, 2], "float32"),
+    "ki": ("sbuf", [128, 24], "int32"), "ni": ("sbuf", [128, 24], "int32"), "ii": ("sbuf", [128, 24], "int32"),
+    "nl": ("sbuf", [128, 24], "uint16"), "il": ("sbuf", [128, 24], "uint16"), "sl": ("sbuf", [128, 24], "uint16"),
+    "ol": ("sbuf", [128, 24], "uint16"), "al": ("sbuf", [128, 24], "uint16"),
+    "f1": ("sbuf", [128, 24], "float32"), "f2": ("sbuf", [128, 24], "float32"), "f3": ("sbuf", [128, 24], "float32"),
+    "g0": ("sbuf", [128, 24], "float32"), "g1": ("sbuf", [128, 24], "float32"), "g2": ("sbuf", [128, 24], "float32"),
+    "g3": ("sbuf", [128, 24], "float32"), "g4": ("sbuf", [128, 24], "float32"), "g5": ("sbuf", [128, 24], "float32"),
+    "g6": ("sbuf", [128, 24], "float32"), "basev": ("sbuf", [128, 24], "float32"), "ho": ("sbuf", [128, 24], "float32"),
+    "x1": ("sbuf", [128, L], "float32"), "xx": ("sbuf", [128, L], "bfloat16"), "xt": ("sbuf", [128, L], "bfloat16"),
+    "ng": ("sbuf", [128, L], "bfloat16"), "nd": ("sbuf", [128, L], "bfloat16"), "wv": ("sbuf", [128, L], "bfloat16"),
+    "nh": ("sbuf", [128, L], "float16"), "ag": ("sbuf", [128, L], "bfloat16"), "p0": ("sbuf", [128, L], "float32"),
+    "ab": ("sbuf", [128, L], "float32"), "th": ("sbuf", [128, L], "bfloat16"), "tn": ("sbuf", [128, L], "bfloat16"),
+    "td": ("sbuf", [128, L], "bfloat16"), "pp": ("sbuf", [128, L], "float32"), "st": ("sbuf", [128, L], "float32"),
+    "ss": ("sbuf", [128, L], "float16"), "qn": ("sbuf", [128, L], "float32"), "q2": ("sbuf", [128, L], "float32"),
+    "ps0": ("psum", [128, 512], "float32"), "ps1": ("psum", [128, 512], "float32"), "ps2": ("psum", [128, 512], "float32"),
+    "key0": ("psum", [128, 512], "float32"), "key1": ("psum", [128, 512], "float32"), "cv": ("psum", [128, 512], "float32"),
+    "rb": ("psum", [128, 512], "float32"), "k1": ("psum", [128, 12, 2, 16], "float32"),
+}
+SEMAPHORES = ["qv", "qa", "qt", "qp", "dwk", "dvp", "dqu", "dam", "dpay", "dyv", "dyw", "dyc", "arr0", "arr1", "arr2", "sent"]
+
+
+def make_queues(g, T):
+    ops, last_w, readers = [], {}, {}
+
+    def op(q, fn, r=(), w=(), dma=None, ext=None):
+        deps = [(last_w[k], "raw") for k in r if k in last_w]
+        for k in w:
+            if k in last_w:
+                deps.append((last_w[k], "waw"))
+            deps += [(o, "war") for o in readers.get(k, ())]
+        i = len(ops)
+        ops.append({"q": q, "fn": fn, "deps": deps, "dma": dma, "ext": ext, "inc": False})
+        for k in w:
+            last_w[k] = i
+            readers[k] = []
+        for k in r:
+            readers.setdefault(k, []).append(i)
+
+    def emit():
+        engine = {"v": g.vector, "a": g.scalar, "t": g.tensor, "p": g, "s": g.sync}
+        sem = {"v": T.sem.qv, "a": T.sem.qa, "t": T.sem.qt, "p": T.sem.qp}
+        known = {q: {} for q in engine}
+        seq = {q: 0 for q in engine}
+        waits = []
+        for o in ops:
+            o["seq"] = seq[o["q"]]
+            if o["ext"] is None:
+                seq[o["q"]] += 1
+            need = {}
+            kn = known[o["q"]]
+            for j, kind in o["deps"]:
+                d = ops[j]
+                if d["ext"] is not None or d["dma"] is not None:
+                    name = d["ext"] or d["dma"]
+                    if kn.get(name[0], 0) < name[1]:
+                        need[name[0]] = (max(need.get(name[0], (0, 0))[0], name[1]), j)
+                    continue
+                if d["q"] == o["q"] and o["dma"] is None and (kind == "war" or o["q"] == "t"):
+                    continue
+                if kn.get(d["q"], -1) < d["seq"] and need.get(d["q"], (-1, 0))[0] < d["seq"]:
+                    need[d["q"]] = (d["seq"], j)
+            for key, (val, j) in need.items():
+                for k2, v2 in ops[j]["clock"].items():
+                    if k2 != key and kn.get(k2, -1) < v2:
+                        kn[k2] = v2
+            final = []
+            for key, (val, j) in need.items():
+                if not any(k2 != key and ops[j2]["clock"].get(key, -1) >= val for k2, (v2, j2) in need.items()):
+                    final.append((key, val, j))
+                    if key in sem:
+                        ops[j]["inc"] = True
+                kn[key] = max(kn.get(key, -1), val)
+            o["clock"] = dict(kn)
+            waits.append(final)
+        count = {q: 0 for q in engine}
+        for o in ops:
+            count[o["q"]] += 1 if o["inc"] else 0
+            o["count"] = count[o["q"]]
+        for i, o in enumerate(ops):
+            if o["ext"] is not None:
+                continue
+            e = engine[o["q"]]
+            for key, val, j in waits[i]:
+                e.wait_ge(sem[key] if key in sem else T.sem[key], ops[j]["count"] if key in sem else val)
+            ins = o["fn"](e)
+            if o["dma"] is not None:
+                ins.then_inc(T.sem[o["dma"][0]], 16)
+            elif o["inc"]:
+                ins.then_inc(sem[o["q"]], 1)
+        for q in sem:
+            if count[q]:
+                g.wait_ge(sem[q], count[q])
+    return op, emit
+
+
+def rank_program(g, core, T, topo):
+    rank = T.rank_of(core)
+    if rank is None:
+        return
+    op, emit = make_queues(g, T)
+    c_m, c_g, c_p, c_x, c_h0, c_h1, c_ctr, c_sub, c_sgn, c_ini, c_i13, c_n13, c_wn, c_t = range(14)
+
+    def col(k):
+        return T.col[:, k:k + 1]
+
+    def ts(out, in0, s1, s2, o0, o1, r, w):
+        op("v", (lambda e: e.tensor_scalar(out, in0, s1, s2, o0, o1)) if o1 else (lambda e: e.tensor_scalar(out, in0, s1, None, o0)), r, w)
+
+    def tt(out, in0, in1, o, r, w):
+        op("v", lambda e: e.tensor_tensor(out, in0, in1, o), r, w)
+
+    def tc(out, in_, r, w):
+        op("v", lambda e: e.tensor_copy(out, in_), r, w)
+
+    def fill(out, k, w):
+        op("v", lambda e: e.memset(out, k), [], w)
+
+    def act(out, in_, f, r, w, bias=0.0, scale=1.0):
+        op("a", lambda e: e.activation(out, in_, f, bias=bias, scale=scale), r, w)
+
+    def mm(out, lhs, rhs, start, stop, r, w):
+        op("t", lambda e: e.matmul(out, lhs, rhs, start, stop), r, w)
+
+    def iota(out, pattern, base, cm, w):
+        op("p", lambda e: e.iota(out, pattern, base, cm, allow_small_or_imprecise_dtypes=True), [], w)
+
+    fill(T.wkz[:], 0, ["wkz"])
+    op("s", lambda e: e.dma_start(T.wkz[0::16, :], T.wk[:]), [], ["wkz"], dma=("dwk", 16))
+    op("s", lambda e: e.dma_start(T.qw[:, 0:B], T.qu[:]), [], ["qw"], dma=("dqu", 16))
+    op("a", lambda e: e.dma_start(T.vw[:, 0:B], T.vp[:]), [], ["vw"], dma=("dvp", 16))
+    op("a", lambda e: e.dma_start(T.aw[:, 0:W], T.am[:]), [], ["aw"], dma=("dam", 16))
+    for j in range(16):
+        op("s", lambda e, j=j: e.dma_start(T.pw[j::16, :], T.pay[:]), ["aw"] if j == 0 else [], ["pw%d" % j], dma=("dpay", 256))
+
+    op("p", lambda e: e.iota(T.pi[:, 0:1], [[1, 1]], 0, 1), [], ["pi0"])
+    iota(T.iog[:], [[1, 8], [0, 16]], 0, 0, ["iog"])
+    iota(T.io128[:], [[1, 128]], 0, 0, ["io128"])
+    iota(T.io16[:], [[1, 16]], 0, 0, ["io16"])
+    iota(T.trv[:], [[16, 24]], 2064, 1, ["trv"])
+    iota(T.ir[:], [[1, 128], [0, 16]], 0, 0, ["ir"])
+    iota(T.hw[:, 0:4096], [[2, 4096]], -4096, 0, ["hw"])
+    iota(T.hw[:, 4096:W - 1], [[2, W - 1 - 4096]], -2047, 0, ["hwb"])
+    iota(T.hw[:, W - 1:W], [[1, 1]], 5000, 0, ["hwc"])
+    for s in range(RO):
+        for d in range(NR):
+            a0 = PITCH * d + 1
+            iota(T["sw%d" % s][:, a0:a0 + CAP], [[0, CAP]], (d * B + B) * 512, 0, ["sw%d_%d" % (s, d)])
+    fill(T.vw[:, B:B + 16], 0.0, ["vwp"])
+    fill(T.qw[:, B:B + 16], W - 1, ["qwp"])
+    fill(T.zb[:], 0.0, ["zb"])
+    fill(T.lm[:], 0.0, ["lm0"])
+    fill(T.wn[:, 16:32], 0.0, ["wnb"])
+    ts(T.pi[:, 1:2], T.pi[:, 0:1], 15, None, A.bitwise_and, None, ["pi0"], ["pi1"])
+    ts(T.pi[:, 2:3], T.pi[:, 0:1], 4, None, A.arith_shift_right, None, ["pi0"], ["pi2"])
+    ts(T.pi[:, 3:4], T.pi[:, 0:1], 4, 1, A.arith_shift_right, A.bitwise_and, ["pi0"], ["pi3"])
+    tc(col(c_p), T.pi[:, 0:1], ["pi0"], ["c_p"])
+    tc(col(c_m), T.pi[:, 1:2], ["pi1"], ["c_m"])
+    tc(col(c_g), T.pi[:, 2:3], ["pi2"], ["c_g"])
+    tc(col(c_h1), T.pi[:, 3:4], ["pi3"], ["c_h1"])
+    ts(col(c_h0), col(c_h1), -1.0, 1.0, A.mult, A.add, ["c_h1"], ["c_h0"])
+    ts(col(c_x), col(c_h1), -32.0, 16.0, A.mult, A.add, ["c_h1"], ["c_x0"])
+    ts(T.bo[:], T.iog[:], col(c_g), None, A.is_equal, None, ["iog", "c_g"], ["bo"])
+    tt(col(c_x), col(c_x), col(c_p), A.add, ["c_x0", "c_p"], ["c_x"])
+    for k, (pc, hc) in enumerate(((c_p, c_h0), (c_x, c_h0), (c_p, c_h1), (c_x, c_h1))):
+        ts(T.dsf[:, k, :], T.io128[:], col(pc), col(hc), A.is_equal, A.mult, ["io128", "c_p", "c_x", "c_h0", "c_h1"], ["dsf%d" % k])
+    for k in range(4):
+        tc(T.dsb[:, k, :], T.dsf[:, k, :], ["dsf%d" % k], ["dsb%d" % k])
+    dsf = ["dsf%d" % k for k in range(4)]
+    dsb = ["dsb%d" % k for k in range(4)]
+    tc(T.w16[:], T.wkz[:], ["wkz"], ["w16"])
+    tc(T.tt[:], T.wkz[:], ["wkz"], ["tt"])
+    op("v", lambda e: e.transpose(T.yy[:], T.tt[:]), ["tt"], ["yy"])
+    tc(T.tq[:], T.yy[:, 0::16], ["yy"], ["tq"])
+
+    def constants():
+        ts(T.idb[:], T.io128[:], col(c_p), None, A.is_equal, None, ["io128", "c_p"], ["idb"])
+        for a in range(16):
+            ts(T.lm[:, a, a::16], T.bo[:, 0::16], SC, None, A.mult, None, ["bo", "lm0"], ["lm%d" % (a + 1)])
+        ts(col(c_i13), col(c_m), 8192.0, None, A.mult, None, ["c_m"], ["c_i13"])
+        ts(col(c_n13), col(c_m), -8192.0, None, A.mult, None, ["c_m"], ["c_n13"])
+        ts(col(c_wn), col(c_m), 8192.0, float(W - 1), A.mult, A.add, ["c_m"], ["c_wn"])
+        ts(col(c_ctr), col(c_m), -2048.0, -1023.5, A.mult, A.add, ["c_m"], ["c_ctr"])
+        ts(col(c_ini), col(c_m), float(PITCH), -1592.0, A.mult, A.add, ["c_m"], ["c_ini"])
+        ts(col(c_sgn), col(c_m), 8.0, -2.0, A.is_equal, A.mult, ["c_m"], ["c_sgn0"])
+        ts(col(c_t), col(c_m), 8.0, 999.0, A.is_gt, A.mult, ["c_m"], ["c_t"])
+        ts(col(c_sub), col(c_m), 8.0, -1.25, A.is_equal, A.mult, ["c_m"], ["c_sub0"])
+        ts(T.wc[:, 0:16], T.io16[:], col(c_m), None, A.is_gt, None, ["io16", "c_m"], ["wc0"])
+        ts(T.wc[:, 16:32], T.io16[:], col(c_m), -0.5, A.is_equal, A.mult, ["io16", "c_m"], ["wc1"])
+        tc(T.bp[:], T.bo[:], ["bo"], ["bp0"])
+        ts(T.wn[:, 0:16], T.io16[:], col(c_m), col(c_wn), A.is_equal, A.mult, ["io16", "c_m", "c_wn"], ["wna"])
+        ts(col(c_sgn), col(c_sgn), 1.0, None, A.add, None, ["c_sgn0"], ["c_sgn"])
+        tt(col(c_sub), col(c_sub), col(c_t), A.add, ["c_sub0", "c_t"], ["c_sub1"])
+        tt(T.wc[:, 32:48], T.wc[:, 0:16], T.wc[:, 16:32], A.add, ["wc0", "wc1"], ["wc"])
+        ts(T.bp[:, 8::16], T.bo[:, 8::16], -1.0, None, A.mult, None, ["bo", "bp0"], ["bp"])
+        ts(col(c_sub), col(c_sub), 1.0, None, A.add, None, ["c_sub1"], ["c_sub"])
+        for a in range(16):
+            ts(T.tm[:, a, :], T.bp[:], T.wc[:, 32 + a:33 + a], None, A.mult, None, ["bp", "wc"], ["tm%d" % a])
+        ts(T.rm[:], T.ir[:], col(c_p), None, A.is_equal, None, ["ir", "c_p"], ["rm"])
+
+    lms = ["lm%d" % a for a in range(17)]
+    tms = ["tm%d" % a for a in range(16)]
+    ees = ["ee%d" % c for c in range(24)]
+
+    def compare(buf, own, key, own_key):
+        for c in range(24):
+            ts(T.ee[:, c, 0:L - 16 * c], buf[:, 16 * c:L], own[:, c:c + 1], None, A.is_equal, None, [key, own_key], ["ee%d" % c])
+
+    def pairs():
+        mm(T.rb[:, 0:L], T.lm[:, 15, :], T.zb[:], True, False, lms + ["zb"], ["rb"])
+        for c in range(23):
+            mm(T.rb[:, 16 * (c + 1):L], T.bp[:], T.ee[:, c, 16:L - 16 * c], False, False, ["bp", "ee%d" % c], ["rb"])
+        for a in range(16):
+            mm(T.rb[:, a:L:16], T.tm[:, a, :], T.ee[:, :, a], False, a == 15, tms + ees, ["rb"])
+
+    def spread(src, key, c0):
+        for a in range(16):
+            mm(T.cv[:, c0:c0 + 24], T.lm[:, a, :], src[:, a::16], a == 0, a == 15, lms + [key], ["cv"])
+
+    def gather(u):
+        act(T.gg[:, 512 * u:512 * (u + 1)], T.aw[:, 0:W].indirect(T.q16[:, 32 * u:32 * (u + 1)]), F.Copy, ["aw", "q16"], ["gg%d" % u])
+
+    def addv(u):
+        pk = "ps%d" % (u % 3)
+        mm(T[pk][:], T.idb[:], T.gg[:, 512 * u:512 * (u + 1)], True, False, ["idb", "gg%d" % u], [pk])
+        mm(T[pk][:], T.xt[:, 128 * (u // 4):128 * (u // 4 + 1)], T.rm[:, 512 * (u % 4):512 * (u % 4 + 1)], False, True, ["xt", "rm"], [pk])
+
+    def sign(u):
+        pk = "ps%d" % (u % 3)
+        act(T.cc[:, 2 * u:2 * u + 2, :], T[pk][:], F.Sign, [], [pk, "cc%d" % u, "ccb%d" % u], bias=0.5)
+
+    def score(q):
+        kb, off = "key%d" % (q // 3), 64 * (q % 3)
+        for a in range(16):
+            mm(T[kb][:, off:off + 64], T.lm[:, a, :], T.cc[:, 4 * q:4 * q + 4, 16 * a:16 * a + 16], a == 0, a == 15,
+               lms + ["cc%d" % (2 * q), "cc%d" % (2 * q + 1), "ccb%d" % (2 * q), "ccb%d" % (2 * q + 1)], [kb])
+
+    def best(h):
+        kb, hs, n = "key%d" % h, slice(12 * h, 12 * h + 12), "%d" % h
+        tt(T.kk[:, hs, :], T[kb][:, 0:192], T.k1s[:, hs, :], A.add, ["k1s"], [kb, "kk" + n])
+        tt(T.t8[:, hs, :], T.kk[:, hs, 0:8], T.kk[:, hs, 8:16], A.max, ["kk" + n], ["t8" + n])
+        tt(T.t4[:, hs, :], T.t8[:, hs, 0:4], T.t8[:, hs, 4:8], A.max, ["t8" + n], ["t4" + n])
+        tt(T.t2[:, hs, :], T.t4[:, hs, 0:2], T.t4[:, hs, 2:4], A.max, ["t4" + n], ["t2" + n])
+        tt(T.ki[:, hs], T.t2[:, hs, 0], T.t2[:, hs, 1], A.max, ["t2" + n], ["ki" + n])
+
+    def send(s, to_buf):
+        def fn(e):
+            tr = []
+            for d in range(1, NR):
+                to = (rank + d) % NR
+                dst = T.cores[to]
+                rid, pid, _ = topo.addr(dst)
+                m = sum(1 << x for x in topo.engines(core, dst)[2 * d - 2:2 * d])
+                tr.append(RemoteDMATransfer(dst_ids=[DstId(rid=rid, pnc=pid)], dma_engine_mask=m, remote_sem=T.sem["arr%d" % s],
+                                            srcs=[T["sw%d" % s][:, PITCH * to + 1:PITCH * to + 1 + CAP]],
+                                            dsts=[T[to_buf][:, CAP * rank:CAP * (rank + 1)]]))
+            return e.remote_dma_fused(tr, local_sem=T.sem.sent)
+        return fn
+
+    for s in range(RO):
+        lk = "land%d" % s
+        lks = [lk, lk + "o"]
+        if s:
+            land = T[lk]
+            op("v", lambda e, land=land: e.transpose(T.tt[:], land[:]), lks, ["tt"])
+            ts(T.tqi[:], T.tt[:, 0::16], 1.0 / 512, -float(B * rank), A.mult, A.add, ["tt"], ["tqi"])
+            tc(T.tq[:], T.tqi[:], ["tqi"], ["tq"])
+            act(T.yy[:], land[:], F.Identity, lks, ["yy"], bias=BIG - B * rank, scale=1.0 / 512)
+            tc(T.li[:], land[:], lks, ["li"])
+        else:
+            mm(T.rb[:, 0:L], T.bo[:], T.w16[:], True, True, ["bo", "w16"], ["rb"])
+        for cc in range(2):
+            for k in range(2):
+                mm(T.cv[:, cc:24:2], T.dsb[:, 2 * cc + k, :], T.tq[:, (cc ^ k)::2], k == 0, k == 1, dsb + ["tq"], ["cv"])
+        tc(T.bl[:], T.cv[:, 0:24], [], ["cv", "bl"])
+        act(T.bf[:], T.cv[:, 0:24], F.Copy, [], ["cv", "bf"])
+        if s == 0:
+            constants()
+        tc(T.q16[:], T.qw[:, 0:B + 16].indirect(T.bl[:]), ["qw", "qwp", "bl"], ["q16"])
+        if s:
+            ts(T.ci[:], T.li[:], 511, None, A.bitwise_and, None, ["li"], ["ci"])
+            tt(T.x1[:], T.vw[:, 0:B + 16].indirect(T.bl[:]), T.ci[:], A.subtract, ["vw", "vwp", "bl", "ci"], ["x1"])
+            ts(T.xx[:], T.x1[:], -255.0, None, A.max, None, ["x1"], ["xx"])
+        else:
+            act(T.xx[:], T.vw[:, 0:B + 16].indirect(T.bl[:]), F.Copy, ["vw", "vwp", "bl"], ["xx"])
+        k0 = NA // 4
+        for k in range(k0, 3):
+            mm(T.cv[:, 128 * (k + 1):128 * (k + 2)], T.xx[:, 128 * k:128 * (k + 1)], T.idb[:], True, True, ["xx", "idb"], ["cv"])
+        units = list(range(NA, 12))
+        gather(units[0])
+        act(T.xt[:, 128 * k0:L], T.cv[:, 128 * (k0 + 1):512], F.Copy, [], ["cv", "xt"])
+        gather(units[1])
+        for i in range(16):
+            ts(T.vr[:, i:512 * NA:16], T.xx[:, 0:32 * NA], -1.0, None, A.mult, None, ["xx"], ["vr%d" % i])
+        for c in range(2 * NA):
+            tt(T.cc[:, c, :], T.aw[:, 0:W].indirect(T.q16[:, 16 * c:16 * c + 16]), T.vr[:, 256 * c:256 * c + 256], A.is_ge,
+               ["aw", "q16"] + ["vr%d" % i for i in range(16)], ["cc%d" % (c // 2) if c % 2 else "ccb%d" % (c // 2)])
+        ts(T.qf[:], T.q16[:], col(c_i13), None, A.add, None, ["q16", "c_i13"], ["qf"])
+        if s:
+            ts(T.b16[:], T.yy[:], -BIG, None, A.add, None, ["yy"], ["b16"])
+        else:
+            tc(T.b16[:], T.rb[:, 0:L], [], ["rb", "b16"])
+        op("v", lambda e: e.transpose(T.qt[:], T.qf[:]), ["qf"], ["qt"])
+        ts(T.ng[:], T.xx[:], 0.0, 64.0, A.is_lt, A.add, ["xx"], ["ng"])
+        compare(T.b16, T.bf, "b16", "bf")
+        addv(units[0])
+        for k in range(2, len(units) + 2):
+            if k < len(units):
+                gather(units[k])
+            sign(units[k - 2])
+            if k == K_SCORE:
+                for cc in range(2):
+                    for j in range(2):
+                        gx = 16 * (cc ^ j)
+                        mm(T.k1[:, :, cc, :], T.dsf[:, 2 * cc + j, :], T.qt[:, :, gx:gx + 16], j == 0, j == 1, dsf + ["qt"], ["k1"])
+                for q in range(NA // 2):
+                    score(q)
+                tc(T.k1s[:], T.k1[:], [], ["k1", "k1s"])
+            if k - 1 < len(units):
+                addv(units[k - 1])
+            if k == K_PAIRS:
+                pairs()
+                ts(T.rb[:, 0:L], T.rb[:, 0:L], col(c_sgn), 0.0, A.mult, A.is_lt, ["c_sgn"], ["rb"])
+                tt(T.wv[:], T.ng[:], T.rb[:, 0:L], A.mult, ["ng"], ["rb", "wv"])
+            if k == K_VAL:
+                spread(T.wv, "wv", 48)
+                ts(T.basev[:], T.cv[:, 48:72], 1024.5 * SC, 20000.0, A.is_lt, A.mult, [], ["cv", "basev"])
+                ts(T.f1[:], T.cv[:, 48:72], 0.5 * SC, None, A.is_lt, None, [], ["cv", "f1"])
+                tt(T.f2[:], T.f1[:], T.trv[:], A.mult, ["f1", "trv"], ["f2"])
+                tt(T.f3[:], T.f2[:], T.bf[:], A.max, ["f2", "bf"], ["f3"])
+                tc(T.ol[:], T.f3[:], ["f3"], ["ol"])
+            if units[k - 2] % 2:
+                score(units[k - 2] // 2)
+                if units[k - 2] == 5:
+                    act(T.k1[:], T.xx[:], F.Relu, ["xx"], ["k1"], scale=-1.0)
+                    best(0)
+        best(1)
+        ts(T.ni[:], T.ki[:], 8191, None, A.bitwise_and, None, ["ki0", "ki1"], ["ni"])
+        tc(T.nl[:], T.ni[:], ["ni"], ["nl"])
+        act(T.p0[:], T.pw[:, 0:W].indirect(T.nl[:]), F.Copy, ["pw15", "nl"], ["p0"], scale=512.0)
+        act(T.ag[:], T.aw[:, 0:W].indirect(T.nl[:]), F.Copy, ["aw", "nl"], ["ag"])
+        act(T.ab[:], T.p0[:], F.Abs, ["p0", "c_ctr"], ["ab"], bias=col(c_ctr), scale=1.0 / 512)
+        ts(T.f1[:], T.ni[:], 4096.0, -6143.0, A.is_ge, A.mult, ["ni"], ["f1"])
+        ts(T.f2[:], T.ni[:], 2.0, -4096.0, A.mult, A.add, ["ni"], ["f2"])
+        tc(T.nh[:], T.hw[:].indirect(T.nl[:]), ["hw", "hwb", "hwc", "nl"], ["nh"])
+        tt(T.f3[:], T.f1[:], T.basev[:], A.add, ["f1", "basev"], ["f3"])
+        tt(T.ho[:], T.f3[:], T.f2[:], A.add, ["f3", "f2"], ["ho"])
+        compare(T.nh, T.ho, "nh", "ho")
+        pairs()
+        ts(T.th[:], T.ab[:], 1024.0, col(c_sub), A.is_lt, A.subtract, ["ab", "c_sub"], ["th"])
+        tt(T.k1[:], T.ag[:], T.k1[:], A.min, ["ag"], ["k1"])
+        tt(T.ps2[:, 0:L], T.rb[:, 0:L], T.th[:], A.is_lt, ["th"], ["rb", "ps2"])
+        op("v", lambda e: e.tensor_tensor_scan(T.st[:], T.ps2[:, 0:L], T.zb[:], col(c_ini), A.add, A.add), ["zb", "c_ini"], ["ps2", "st"])
+        tt(T.ss[:], T.st[:], T.ps2[:, 0:L], A.mult, ["st"], ["ps2", "ss"])
+        spread(T.ss, "ss", 24)
+        tt(T.pp[:], T.p0[:], T.k1[:], A.add, ["p0"], ["k1", "pp"])
+        ts(T.sl[:], T.cv[:, 24:48], 1.0 / SC, 1592.0, A.mult, A.add, [], ["cv", "sl"])
+        swk = ["sw%d_%d" % (s, d) for d in range(NR)]
+        tc(T["sw%d" % s][:].indirect(T.sl[:]), T.pp[:], ["sl", "pp"], swk)
+        nk = "land%d" % (s + 1)
+        op("p", send(s, nk), swk, [])
+        op("p", None, [], [nk], ext=("arr%d" % s, 2 * (NR - 1)))
+        if s < RO - 1:
+            act(T.g0[:], T.cv[:, 24:48], F.Sign, [], ["cv", "g0"], bias=-1600.0, scale=1.0 / SC)
+            act(T.g2[:], T.cv[:, 24:48], F.Copy, [], ["cv", "g2"], bias=4535.0, scale=1.0 / SC)
+            act(T.tn[:], T.k1[:], F.Copy, [], ["k1", "tn"], scale=-1.0)
+            act(T.g1[:], T.g0[:], F.Relu, ["g0"], ["g1"])
+            act(T.g4[:], T.g0[:], F.Relu, ["g0"], ["g4"], scale=16.0)
+        a0 = PITCH * rank + 1
+        act(T[nk][:, CAP * rank:CAP * (rank + 1)], T["sw%d" % s][:, a0:a0 + CAP], F.Copy, swk, [nk + "o"])
+        if s < RO - 1:
+            ts(T.ii[:], T.ki[:], 13, 15, A.arith_shift_right, A.bitwise_and, ["ki0", "ki1"], ["ii"])
+            tt(T.g3[:], T.g1[:], T.g2[:], A.mult, ["g1", "g2"], ["g3"])
+            tt(T.g5[:], T.g4[:], T.ii[:], A.add, ["g4", "ii"], ["g5"])
+            tc(T.il[:], T.g5[:], ["g5"], ["il"])
+            tt(T.qn[:], T.wn[:].indirect(T.il[:]), T.qf[:], A.max, ["wna", "wnb", "il", "qf"], ["qn"])
+            act(T.q2[:], T.qn[:], F.Identity, ["qn", "c_n13"], ["q2"], bias=col(c_n13))
+        ts(T.nd[:], T.rb[:, 0:L], col(c_sgn), 0.0, A.mult, A.is_lt, ["c_sgn"], ["rb", "nd"])
+        tt(T.td[:], T.nd[:], T.k1[:], A.mult, ["nd"], ["k1", "td"])
+        if s < RO - 1:
+            tt(T.g6[:], T.g3[:], T.ni[:], A.max, ["g3", "ni"], ["g6"])
+            tc(T.qw[:].indirect(T.ol[:]), T.q2[:], ["ol", "q2"], ["qw", "qwp"])
+            tc(T.al[:], T.g6[:], ["g6"], ["al"])
+        tt(T.vw[:].indirect(T.ol[:]), T.xx[:], T.td[:], A.add, ["ol", "xx", "td"], ["vw", "vwp"])
+        if s < RO - 1:
+            tt(T.aw[:].indirect(T.al[:]), T.ag[:], T.tn[:], A.add, ["al", "ag", "tn"], ["aw"])
+        else:
+            op("s", lambda e: e.dma_start(T.yv[:], T.vw[:, 0:B]), ["vw"], ["yv"], dma=("dyv", 16))
+
+    lk = "land%d" % RO
+    lks = [lk, lk + "o"]
+    act(T.yy[:], T[lk][:], F.Identity, lks, ["yy"], bias=BIG - B * rank, scale=1.0 / 512)
+    act(T.x1[:], T.yy[:], F.Identity, ["yy"], ["x1"], bias=-BIG)
+    op("a", lambda e: e.dma_start(T.yw[:], T.x1[0::16, :]), ["x1"], ["yw"], dma=("dyw", 16))
+    tc(T.li[:], T[lk][:], lks, ["li"])
+    ts(T.ci[:], T.li[:], 511, None, A.bitwise_and, None, ["li"], ["ci"])
+    tc(T.cb[:], T.ci[:], ["ci"], ["cb"])
+    op("s", lambda e: e.dma_start(T.yc[:], T.cb[:]), ["cb"], ["yc"], dma=("dyc", 16))
+    emit()
+    g.wait_ge(T.sem.sent, 2 * (NR - 1) * RO)
+    for n in ("dyv", "dyw", "dyc", "dwk", "dvp", "dqu", "dam"):
+        g.wait_ge(T.sem[n], 16)
+    g.wait_ge(T.sem.dpay, 256)

@@ -12,13 +12,14 @@ SW = 3600
 BIG = 8388608.0
 SC = 131072.0
 NA = 4
-K_SCORE, K_PAIRS, K_VAL = 2, 3, 5
+K_PAIRS, N_PAIRS, K_ND, K_VAL, K_BASE, K_SCORE, K_BEST = 2, 2, 3, 4, 5, 6, 7
+C_OWN = {2: (0, 4), 4: (4, 8)}
 
 SCRATCH = {
     "vw": ("sbuf", [128, VW], "bfloat16"), "qw": ("sbuf", [128, VW], "int32"), "aw": ("sbuf", [128, AW], "bfloat16"),
     "pw": ("sbuf", [128, W], "int32"), "hw": ("sbuf", [128, W], "float32"), "wn": ("sbuf", [128, 32], "float32"),
     "cc": ("sbuf", [128, 24, 256], "bfloat16"), "gg": ("sbuf", [128, L * 16], "bfloat16"),
-    "vr": ("sbuf", [128, L * 16], "bfloat16"), "ee": ("sbuf", [128, 24, L], "bfloat16"),
+    "vr": ("sbuf", [128, 3072], "bfloat16"), "ee": ("sbuf", [128, 24, L], "bfloat16"),
     "lm": ("sbuf", [128, 16, 128], "bfloat16"), "tm": ("sbuf", [128, 16, 128], "bfloat16"),
     "rm": ("sbuf", [128, 2048], "bfloat16"), "ir": ("sbuf", [128, 2048], "bfloat16"),
     "bo": ("sbuf", [128, 128], "bfloat16"), "bp": ("sbuf", [128, 128], "bfloat16"), "idb": ("sbuf", [128, 128], "bfloat16"),
@@ -38,6 +39,7 @@ SCRATCH = {
     "nl": ("sbuf", [128, 24], "uint16"), "il": ("sbuf", [128, 24], "uint16"), "sl": ("sbuf", [128, 24], "uint16"),
     "ol": ("sbuf", [128, 24], "uint16"), "al": ("sbuf", [128, 24], "uint16"),
     "f1": ("sbuf", [128, 24], "float32"), "f2": ("sbuf", [128, 24], "float32"), "f3": ("sbuf", [128, 24], "float32"),
+    "e1": ("sbuf", [128, 24], "float32"), "e2": ("sbuf", [128, 24], "float32"), "e3": ("sbuf", [128, 24], "float32"),
     "g0": ("sbuf", [128, 24], "float32"), "g1": ("sbuf", [128, 24], "float32"), "g2": ("sbuf", [128, 24], "float32"),
     "g3": ("sbuf", [128, 24], "float32"), "g4": ("sbuf", [128, 24], "float32"), "g5": ("sbuf", [128, 24], "float32"),
     "g6": ("sbuf", [128, 24], "float32"), "basev": ("sbuf", [128, 24], "float32"), "ho": ("sbuf", [128, 24], "float32"),
@@ -133,7 +135,7 @@ def rank_program(g, core, T, topo):
     if rank is None:
         return
     op, emit = make_queues(g, T)
-    c_m, c_g, c_p, c_x, c_h0, c_h1, c_ctr, c_sub, c_sgn, c_ini, c_i13, c_n13, c_wn, c_t = range(14)
+    c_m, c_g, c_p, c_x, c_h0, c_h1, c_ctr, c_sub, c_sgn, c_ini, c_i13, c_n13, c_wn, c_t, c_sg2 = range(15)
 
     def col(k):
         return T.col[:, k:k + 1]
@@ -163,7 +165,7 @@ def rank_program(g, core, T, topo):
     op("s", lambda e: e.dma_start(T.wkz[0::16, :], T.wk[:]), [], ["wkz"], dma=("dwk", 16))
     op("s", lambda e: e.dma_start(T.qw[:, 0:B], T.qu[:]), [], ["qw"], dma=("dqu", 16))
     op("a", lambda e: e.dma_start(T.vw[:, 0:B], T.vp[:]), [], ["vw"], dma=("dvp", 16))
-    op("a", lambda e: e.dma_start(T.aw[:, 0:W], T.am[:]), [], ["aw"], dma=("dam", 16))
+    op("s", lambda e: e.dma_start(T.aw[:, 0:W], T.am[:]), [], ["aw"], dma=("dam", 16))
     for j in range(16):
         op("s", lambda e, j=j: e.dma_start(T.pw[j::16, :], T.pay[:]), ["aw"] if j == 0 else [], ["pw%d" % j], dma=("dpay", 256))
 
@@ -202,50 +204,57 @@ def rank_program(g, core, T, topo):
         tc(T.dsb[:, k, :], T.dsf[:, k, :], ["dsf%d" % k], ["dsb%d" % k])
     dsf = ["dsf%d" % k for k in range(4)]
     dsb = ["dsb%d" % k for k in range(4)]
+    ts(T.idb[:], T.io128[:], col(c_p), None, A.is_equal, None, ["io128", "c_p"], ["idb"])
+    for a in range(16):
+        ts(T.lm[:, a, a::16], T.bo[:, 0::16], SC, None, A.mult, None, ["bo", "lm0"], ["lm%d" % (a + 1)])
+    ts(col(c_i13), col(c_m), 8192.0, None, A.mult, None, ["c_m"], ["c_i13"])
+    ts(col(c_n13), col(c_m), -8192.0, None, A.mult, None, ["c_m"], ["c_n13"])
+    ts(col(c_wn), col(c_m), 8192.0, float(W - 1), A.mult, A.add, ["c_m"], ["c_wn"])
+    ts(col(c_ctr), col(c_m), -2048.0, -1023.5, A.mult, A.add, ["c_m"], ["c_ctr"])
+    ts(col(c_ini), col(c_m), float(PITCH), -1592.0, A.mult, A.add, ["c_m"], ["c_ini"])
+    ts(col(c_sgn), col(c_m), 8.0, -2.0, A.is_equal, A.mult, ["c_m"], ["c_sgn0"])
+    ts(col(c_t), col(c_m), 8.0, 999.0, A.is_gt, A.mult, ["c_m"], ["c_t"])
+    ts(col(c_sub), col(c_m), 8.0, -1.25, A.is_equal, A.mult, ["c_m"], ["c_sub0"])
+    ts(T.wc[:, 0:16], T.io16[:], col(c_m), None, A.is_gt, None, ["io16", "c_m"], ["wc0"])
+    ts(T.wc[:, 16:32], T.io16[:], col(c_m), -0.5, A.is_equal, A.mult, ["io16", "c_m"], ["wc1"])
+    tc(T.bp[:], T.bo[:], ["bo"], ["bp0"])
+    ts(T.wn[:, 0:16], T.io16[:], col(c_m), col(c_wn), A.is_equal, A.mult, ["io16", "c_m", "c_wn"], ["wna"])
+    ts(col(c_sgn), col(c_sgn), 1.0, None, A.add, None, ["c_sgn0"], ["c_sgn"])
+    ts(col(c_sg2), col(c_sgn), -2.0, None, A.mult, None, ["c_sgn"], ["c_sg2"])
+    tt(col(c_sub), col(c_sub), col(c_t), A.add, ["c_sub0", "c_t"], ["c_sub1"])
+    tt(T.wc[:, 32:48], T.wc[:, 0:16], T.wc[:, 16:32], A.add, ["wc0", "wc1"], ["wc"])
+    ts(T.bp[:, 8::16], T.bo[:, 8::16], -1.0, None, A.mult, None, ["bo", "bp0"], ["bp"])
+    ts(col(c_sub), col(c_sub), 1.0, None, A.add, None, ["c_sub1"], ["c_sub"])
+    for a in range(16):
+        ts(T.tm[:, a, :], T.bp[:], T.wc[:, 32 + a:33 + a], None, A.mult, None, ["bp", "wc"], ["tm%d" % a])
+    ts(T.rm[:], T.ir[:], col(c_p), None, A.is_equal, None, ["ir", "c_p"], ["rm"])
     tc(T.w16[:], T.wkz[:], ["wkz"], ["w16"])
     tc(T.tt[:], T.wkz[:], ["wkz"], ["tt"])
     op("v", lambda e: e.transpose(T.yy[:], T.tt[:]), ["tt"], ["yy"])
     tc(T.tq[:], T.yy[:, 0::16], ["yy"], ["tq"])
 
-    def constants():
-        ts(T.idb[:], T.io128[:], col(c_p), None, A.is_equal, None, ["io128", "c_p"], ["idb"])
-        for a in range(16):
-            ts(T.lm[:, a, a::16], T.bo[:, 0::16], SC, None, A.mult, None, ["bo", "lm0"], ["lm%d" % (a + 1)])
-        ts(col(c_i13), col(c_m), 8192.0, None, A.mult, None, ["c_m"], ["c_i13"])
-        ts(col(c_n13), col(c_m), -8192.0, None, A.mult, None, ["c_m"], ["c_n13"])
-        ts(col(c_wn), col(c_m), 8192.0, float(W - 1), A.mult, A.add, ["c_m"], ["c_wn"])
-        ts(col(c_ctr), col(c_m), -2048.0, -1023.5, A.mult, A.add, ["c_m"], ["c_ctr"])
-        ts(col(c_ini), col(c_m), float(PITCH), -1592.0, A.mult, A.add, ["c_m"], ["c_ini"])
-        ts(col(c_sgn), col(c_m), 8.0, -2.0, A.is_equal, A.mult, ["c_m"], ["c_sgn0"])
-        ts(col(c_t), col(c_m), 8.0, 999.0, A.is_gt, A.mult, ["c_m"], ["c_t"])
-        ts(col(c_sub), col(c_m), 8.0, -1.25, A.is_equal, A.mult, ["c_m"], ["c_sub0"])
-        ts(T.wc[:, 0:16], T.io16[:], col(c_m), None, A.is_gt, None, ["io16", "c_m"], ["wc0"])
-        ts(T.wc[:, 16:32], T.io16[:], col(c_m), -0.5, A.is_equal, A.mult, ["io16", "c_m"], ["wc1"])
-        tc(T.bp[:], T.bo[:], ["bo"], ["bp0"])
-        ts(T.wn[:, 0:16], T.io16[:], col(c_m), col(c_wn), A.is_equal, A.mult, ["io16", "c_m", "c_wn"], ["wna"])
-        ts(col(c_sgn), col(c_sgn), 1.0, None, A.add, None, ["c_sgn0"], ["c_sgn"])
-        tt(col(c_sub), col(c_sub), col(c_t), A.add, ["c_sub0", "c_t"], ["c_sub1"])
-        tt(T.wc[:, 32:48], T.wc[:, 0:16], T.wc[:, 16:32], A.add, ["wc0", "wc1"], ["wc"])
-        ts(T.bp[:, 8::16], T.bo[:, 8::16], -1.0, None, A.mult, None, ["bo", "bp0"], ["bp"])
-        ts(col(c_sub), col(c_sub), 1.0, None, A.add, None, ["c_sub1"], ["c_sub"])
-        for a in range(16):
-            ts(T.tm[:, a, :], T.bp[:], T.wc[:, 32 + a:33 + a], None, A.mult, None, ["bp", "wc"], ["tm%d" % a])
-        ts(T.rm[:], T.ir[:], col(c_p), None, A.is_equal, None, ["ir", "c_p"], ["rm"])
-
     lms = ["lm%d" % a for a in range(17)]
     tms = ["tm%d" % a for a in range(16)]
-    ees = ["ee%d" % c for c in range(24)]
+    ees = ["ee%d" % c for c in range(24)] + ["ee%dx" % c for c in range(12)]
 
-    def compare(buf, own, key, own_key):
-        for c in range(24):
-            ts(T.ee[:, c, 0:L - 16 * c], buf[:, 16 * c:L], own[:, c:c + 1], None, A.is_equal, None, [key, own_key], ["ee%d" % c])
+    def compare(buf, own, key, own_key, h=None):
+        for c in range(12 if h == 0 else 24):
+            lo = 192 if h == 1 and c < 12 else 16 * c
+            hi = 192 if h == 0 else L
+            ts(T.ee[:, c, lo - 16 * c:hi - 16 * c], buf[:, lo:hi], own[:, c:c + 1], None, A.is_equal, None,
+               [key + "0" if h is not None else key, own_key + "0" if c < 12 and h is not None else own_key] + ([key] if h == 1 else []),
+               ["ee%d%s" % (c, "x" if h == 0 else "")])
 
-    def pairs():
-        mm(T.rb[:, 0:L], T.lm[:, 15, :], T.zb[:], True, False, lms + ["zb"], ["rb"])
+    def pairs(part=0, parts=1):
+        calls = [lambda: mm(T.rb[:, 0:L], T.lm[:, 15, :], T.zb[:], True, False, lms + ["zb"], ["rb"])]
         for c in range(23):
-            mm(T.rb[:, 16 * (c + 1):L], T.bp[:], T.ee[:, c, 16:L - 16 * c], False, False, ["bp", "ee%d" % c], ["rb"])
+            calls.append(lambda c=c: mm(T.rb[:, 16 * (c + 1):L], T.bp[:], T.ee[:, c, 16:L - 16 * c], False, False,
+                                        ["bp", "ee%d" % c] + (["ee%dx" % c] if c < 12 else []), ["rb"]))
         for a in range(16):
-            mm(T.rb[:, a:L:16], T.tm[:, a, :], T.ee[:, :, a], False, a == 15, tms + ees, ["rb"])
+            calls.append(lambda a=a: mm(T.rb[:, a:L:16], T.tm[:, a, :], T.ee[:, :, a], False, a == 15, tms + ees, ["rb"]))
+        n = len(calls)
+        for f in calls[n * part // parts:n * (part + 1) // parts]:
+            f()
 
     def spread(src, key, c0):
         for a in range(16):
@@ -277,14 +286,33 @@ def rank_program(g, core, T, topo):
         tt(T.t2[:, hs, :], T.t4[:, hs, 0:2], T.t4[:, hs, 2:4], A.max, ["t4" + n], ["t2" + n])
         tt(T.ki[:, hs], T.t2[:, hs, 0], T.t2[:, hs, 1], A.max, ["t2" + n], ["ki" + n])
 
+    def own_units(c0, c1):
+        for c in range(c0, c1):
+            tt(T.cc[:, c, :], T.aw[:, 0:W].indirect(T.q16[:, 16 * c:16 * c + 16]), T.vr[:, 256 * c:256 * c + 256], A.is_ge,
+               ["aw", "q16"] + ["vr%d" % i for i in range(16)], ["cc%d" % (c // 2) if c % 2 else "ccb%d" % (c // 2)])
+
+    def lines(h):
+        hs, n, ls = slice(12 * h, 12 * h + 12), "%d" % h, slice(192 * h, 192 * h + 192)
+        ts(T.ni[:, hs], T.ki[:, hs], 8191, None, A.bitwise_and, None, ["ki" + n], ["ni" + n])
+        tc(T.nl[:, hs], T.ni[:, hs], ["ni" + n], ["nl" + n])
+        ts(T.f1[:, hs], T.ni[:, hs], 4096.0, -6143.0, A.is_ge, A.mult, ["ni" + n], ["f1" + n])
+        ts(T.f2[:, hs], T.ni[:, hs], 2.0, -4096.0, A.mult, A.add, ["ni" + n], ["f2" + n])
+        tc(T.nh[:, ls], T.hw[:].indirect(T.nl[:, hs]), ["hw", "hwb", "hwc", "nl" + n], ["nh" + n if h == 0 else "nh"])
+        tt(T.f3[:, hs], T.f1[:, hs], T.basev[:, hs], A.add, ["f1" + n, "basev"], ["f3" + n])
+        tt(T.ho[:, hs], T.f3[:, hs], T.f2[:, hs], A.add, ["f3" + n, "f2" + n], ["ho" + n if h == 0 else "ho"])
+
     def send(s, to_buf):
         def fn(e):
             tr = []
+            nth = [0, 0]
             for d in range(1, NR):
                 to = (rank + d) % NR
                 dst = T.cores[to]
                 rid, pid, _ = topo.addr(dst)
-                m = sum(1 << x for x in topo.engines(core, dst)[2 * d - 2:2 * d])
+                near = int(topo.die(dst) == topo.die(core))
+                k = 4 * nth[near] + near
+                nth[near] += 1
+                m = sum(1 << x for x in topo.engines(core, dst)[k:k + 3:2])
                 tr.append(RemoteDMATransfer(dst_ids=[DstId(rid=rid, pnc=pid)], dma_engine_mask=m, remote_sem=T.sem["arr%d" % s],
                                             srcs=[T["sw%d" % s][:, PITCH * to + 1:PITCH * to + 1 + CAP]],
                                             dsts=[T[to_buf][:, CAP * rank:CAP * (rank + 1)]]))
@@ -308,9 +336,13 @@ def rank_program(g, core, T, topo):
                 mm(T.cv[:, cc:24:2], T.dsb[:, 2 * cc + k, :], T.tq[:, (cc ^ k)::2], k == 0, k == 1, dsb + ["tq"], ["cv"])
         tc(T.bl[:], T.cv[:, 0:24], [], ["cv", "bl"])
         act(T.bf[:], T.cv[:, 0:24], F.Copy, [], ["cv", "bf"])
-        if s == 0:
-            constants()
         tc(T.q16[:], T.qw[:, 0:B + 16].indirect(T.bl[:]), ["qw", "qwp", "bl"], ["q16"])
+        ts(T.qf[:], T.q16[:], col(c_i13), None, A.add, None, ["q16", "c_i13"], ["qf"])
+        op("v", lambda e: e.transpose(T.qt[:], T.qf[:]), ["qf"], ["qt"])
+        for cc in range(2):
+            for j in range(2):
+                gx = 16 * (cc ^ j)
+                mm(T.k1[:, :, cc, :], T.dsf[:, 2 * cc + j, :], T.qt[:, :, gx:gx + 16], j == 0, j == 1, dsf + ["qt"], ["k1"])
         if s:
             ts(T.ci[:], T.li[:], 511, None, A.bitwise_and, None, ["li"], ["ci"])
             tt(T.x1[:], T.vw[:, 0:B + 16].indirect(T.bl[:]), T.ci[:], A.subtract, ["vw", "vwp", "bl", "ci"], ["x1"])
@@ -322,64 +354,54 @@ def rank_program(g, core, T, topo):
             mm(T.cv[:, 128 * (k + 1):128 * (k + 2)], T.xx[:, 128 * k:128 * (k + 1)], T.idb[:], True, True, ["xx", "idb"], ["cv"])
         units = list(range(NA, 12))
         gather(units[0])
-        act(T.xt[:, 128 * k0:L], T.cv[:, 128 * (k0 + 1):512], F.Copy, [], ["cv", "xt"])
         gather(units[1])
-        for i in range(16):
-            ts(T.vr[:, i:512 * NA:16], T.xx[:, 0:32 * NA], -1.0, None, A.mult, None, ["xx"], ["vr%d" % i])
-        for c in range(2 * NA):
-            tt(T.cc[:, c, :], T.aw[:, 0:W].indirect(T.q16[:, 16 * c:16 * c + 16]), T.vr[:, 256 * c:256 * c + 256], A.is_ge,
-               ["aw", "q16"] + ["vr%d" % i for i in range(16)], ["cc%d" % (c // 2) if c % 2 else "ccb%d" % (c // 2)])
-        ts(T.qf[:], T.q16[:], col(c_i13), None, A.add, None, ["q16", "c_i13"], ["qf"])
+        act(T.xt[:, 128 * k0:L], T.cv[:, 128 * (k0 + 1):512], F.Copy, [], ["cv", "xt"])
         if s:
             ts(T.b16[:], T.yy[:], -BIG, None, A.add, None, ["yy"], ["b16"])
         else:
             tc(T.b16[:], T.rb[:, 0:L], [], ["rb", "b16"])
-        op("v", lambda e: e.transpose(T.qt[:], T.qf[:]), ["qf"], ["qt"])
         ts(T.ng[:], T.xx[:], 0.0, 64.0, A.is_lt, A.add, ["xx"], ["ng"])
         compare(T.b16, T.bf, "b16", "bf")
+        for i in range(16):
+            ts(T.vr[:, i:512 * NA:16], T.xx[:, 0:32 * NA], -1.0, None, A.mult, None, ["xx"], ["vr%d" % i])
         addv(units[0])
         for k in range(2, len(units) + 2):
             if k < len(units):
                 gather(units[k])
             sign(units[k - 2])
-            if k == K_SCORE:
-                for cc in range(2):
-                    for j in range(2):
-                        gx = 16 * (cc ^ j)
-                        mm(T.k1[:, :, cc, :], T.dsf[:, 2 * cc + j, :], T.qt[:, :, gx:gx + 16], j == 0, j == 1, dsf + ["qt"], ["k1"])
-                for q in range(NA // 2):
-                    score(q)
-                tc(T.k1s[:], T.k1[:], [], ["k1", "k1s"])
             if k - 1 < len(units):
                 addv(units[k - 1])
-            if k == K_PAIRS:
-                pairs()
+            own_units(*C_OWN.get(k, (0, 0)))
+            if K_PAIRS <= k < K_PAIRS + N_PAIRS:
+                pairs(k - K_PAIRS, N_PAIRS)
+            if k == K_ND:
                 ts(T.rb[:, 0:L], T.rb[:, 0:L], col(c_sgn), 0.0, A.mult, A.is_lt, ["c_sgn"], ["rb"])
                 tt(T.wv[:], T.ng[:], T.rb[:, 0:L], A.mult, ["ng"], ["rb", "wv"])
             if k == K_VAL:
                 spread(T.wv, "wv", 48)
+            if k == K_BASE:
                 ts(T.basev[:], T.cv[:, 48:72], 1024.5 * SC, 20000.0, A.is_lt, A.mult, [], ["cv", "basev"])
-                ts(T.f1[:], T.cv[:, 48:72], 0.5 * SC, None, A.is_lt, None, [], ["cv", "f1"])
-                tt(T.f2[:], T.f1[:], T.trv[:], A.mult, ["f1", "trv"], ["f2"])
-                tt(T.f3[:], T.f2[:], T.bf[:], A.max, ["f2", "bf"], ["f3"])
-                tc(T.ol[:], T.f3[:], ["f3"], ["ol"])
+                ts(T.e1[:], T.cv[:, 48:72], 0.5 * SC, None, A.is_lt, None, [], ["cv", "e1"])
+                tt(T.e2[:], T.e1[:], T.trv[:], A.mult, ["e1", "trv"], ["e2"])
+                tt(T.e3[:], T.e2[:], T.bf[:], A.max, ["e2", "bf"], ["e3"])
+                tc(T.ol[:], T.e3[:], ["e3"], ["ol"])
+            if k == K_SCORE:
+                for q in range(NA // 2):
+                    score(q)
+                tc(T.k1s[:], T.k1[:], [], ["k1", "k1s"])
             if units[k - 2] % 2:
                 score(units[k - 2] // 2)
-                if units[k - 2] == 5:
-                    act(T.k1[:], T.xx[:], F.Relu, ["xx"], ["k1"], scale=-1.0)
-                    best(0)
+            if k == K_BEST:
+                best(0)
+                lines(0)
+                compare(T.nh, T.ho, "nh", "ho", 0)
+        act(T.k1[:], T.xx[:], F.Relu, ["xx"], ["k1"], scale=-1.0)
         best(1)
-        ts(T.ni[:], T.ki[:], 8191, None, A.bitwise_and, None, ["ki0", "ki1"], ["ni"])
-        tc(T.nl[:], T.ni[:], ["ni"], ["nl"])
-        act(T.p0[:], T.pw[:, 0:W].indirect(T.nl[:]), F.Copy, ["pw15", "nl"], ["p0"], scale=512.0)
-        act(T.ag[:], T.aw[:, 0:W].indirect(T.nl[:]), F.Copy, ["aw", "nl"], ["ag"])
+        lines(1)
+        act(T.p0[:], T.pw[:, 0:W].indirect(T.nl[:]), F.Copy, ["pw15", "nl0", "nl1"], ["p0"], scale=512.0)
+        act(T.ag[:], T.aw[:, 0:W].indirect(T.nl[:]), F.Copy, ["aw", "nl0", "nl1"], ["ag"])
         act(T.ab[:], T.p0[:], F.Abs, ["p0", "c_ctr"], ["ab"], bias=col(c_ctr), scale=1.0 / 512)
-        ts(T.f1[:], T.ni[:], 4096.0, -6143.0, A.is_ge, A.mult, ["ni"], ["f1"])
-        ts(T.f2[:], T.ni[:], 2.0, -4096.0, A.mult, A.add, ["ni"], ["f2"])
-        tc(T.nh[:], T.hw[:].indirect(T.nl[:]), ["hw", "hwb", "hwc", "nl"], ["nh"])
-        tt(T.f3[:], T.f1[:], T.basev[:], A.add, ["f1", "basev"], ["f3"])
-        tt(T.ho[:], T.f3[:], T.f2[:], A.add, ["f3", "f2"], ["ho"])
-        compare(T.nh, T.ho, "nh", "ho")
+        compare(T.nh, T.ho, "nh", "ho", 1)
         pairs()
         ts(T.th[:], T.ab[:], 1024.0, col(c_sub), A.is_lt, A.subtract, ["ab", "c_sub"], ["th"])
         tt(T.k1[:], T.ag[:], T.k1[:], A.min, ["ag"], ["k1"])
@@ -400,6 +422,7 @@ def rank_program(g, core, T, topo):
             act(T.tn[:], T.k1[:], F.Copy, [], ["k1", "tn"], scale=-1.0)
             act(T.g1[:], T.g0[:], F.Relu, ["g0"], ["g1"])
             act(T.g4[:], T.g0[:], F.Relu, ["g0"], ["g4"], scale=16.0)
+        act(T.nd[:], T.rb[:, 0:L], F.Relu, ["c_sg2"], ["rb", "nd"], scale=col(c_sg2))
         a0 = PITCH * rank + 1
         act(T[nk][:, CAP * rank:CAP * (rank + 1)], T["sw%d" % s][:, a0:a0 + CAP], F.Copy, swk, [nk + "o"])
         if s < RO - 1:
@@ -409,10 +432,9 @@ def rank_program(g, core, T, topo):
             tc(T.il[:], T.g5[:], ["g5"], ["il"])
             tt(T.qn[:], T.wn[:].indirect(T.il[:]), T.qf[:], A.max, ["wna", "wnb", "il", "qf"], ["qn"])
             act(T.q2[:], T.qn[:], F.Identity, ["qn", "c_n13"], ["q2"], bias=col(c_n13))
-        ts(T.nd[:], T.rb[:, 0:L], col(c_sgn), 0.0, A.mult, A.is_lt, ["c_sgn"], ["rb", "nd"])
         tt(T.td[:], T.nd[:], T.k1[:], A.mult, ["nd"], ["k1", "td"])
         if s < RO - 1:
-            tt(T.g6[:], T.g3[:], T.ni[:], A.max, ["g3", "ni"], ["g6"])
+            tt(T.g6[:], T.g3[:], T.ni[:], A.max, ["g3", "ni0", "ni1"], ["g6"])
             tc(T.qw[:].indirect(T.ol[:]), T.q2[:], ["ol", "q2"], ["qw", "qwp"])
             tc(T.al[:], T.g6[:], ["g6"], ["al"])
         tt(T.vw[:].indirect(T.ol[:]), T.xx[:], T.td[:], A.add, ["ol", "xx", "td"], ["vw", "vwp"])

from concourse.bass import DstId, RemoteDMATransfer
from concourse.mybir import AluOpType, ActivationFunctionType

A = AluOpType
F = ActivationFunctionType
NR, B, W, CAP, RO = 8, 2048, 6144, 48, 3
L = NR * CAP
VW = 2560
AW = 6544
PITCH = 400
SW = 3600
BIG = 8388608.0
SC = 131072.0
NA = 4
K_PAIRS, N_PAIRS, K_ND, K_VAL, K_BASE, K_SCORE, K_BEST = 2, 2, 3, 4, 5, 6, 7
C_OWN = {2: (0, 4), 4: (4, 8)}

SCRATCH = {
    "vw": ("sbuf", [128, VW], "bfloat16"), "qw": ("sbuf", [128, VW], "int32"), "aw": ("sbuf", [128, AW], "bfloat16"),
    "pw": ("sbuf", [128, W], "int32"), "hw": ("sbuf", [128, W], "float32"), "wn": ("sbuf", [128, 32], "float32"),
    "cc": ("sbuf", [128, 24, 256], "bfloat16"), "gg": ("sbuf", [128, L * 16], "bfloat16"),
    "vr": ("sbuf", [128, 3072], "bfloat16"), "ee": ("sbuf", [128, 24, L], "bfloat16"),
    "lm": ("sbuf", [128, 16, 128], "bfloat16"), "tm": ("sbuf", [128, 16, 128], "bfloat16"),
    "rm": ("sbuf", [128, 2048], "bfloat16"), "ir": ("sbuf", [128, 2048], "bfloat16"),
    "bo": ("sbuf", [128, 128], "bfloat16"), "bp": ("sbuf", [128, 128], "bfloat16"), "idb": ("sbuf", [128, 128], "bfloat16"),
    "zb": ("sbuf", [128, L], "bfloat16"), "dsf": ("sbuf", [128, 4, 128], "float32"), "dsb": ("sbuf", [128, 4, 128], "bfloat16"),
    "pi": ("sbuf", [128, 4], "int32"), "io128": ("sbuf", [128, 128], "bfloat16"), "iog": ("sbuf", [128, 128], "bfloat16"),
    "io16": ("sbuf", [128, 16], "bfloat16"), "trv": ("sbuf", [128, 24], "float32"), "wc": ("sbuf", [128, 48], "float32"),
    "col": ("sbuf", [128, 16], "float32"), "wkz": ("sbuf", [128, L], "int32"), "w16": ("sbuf", [128, L], "float16"),
    "land1": ("sbuf", [128, L], "float32"), "land2": ("sbuf", [128, L], "float32"), "land3": ("sbuf", [128, L], "float32"),
    "sw0": ("sbuf", [128, SW], "float32"), "sw1": ("sbuf", [128, SW], "float32"), "sw2": ("sbuf", [128, SW], "float32"),
    "tt": ("sbuf", [128, L], "float32"), "tqi": ("sbuf", [128, 24], "int32"), "tq": ("sbuf", [128, 24], "float16"),
    "bl": ("sbuf", [128, 24], "uint16"), "bf": ("sbuf", [128, 24], "float32"), "b16": ("sbuf", [128, L], "float16"),
    "yy": ("sbuf", [128, L], "float32"), "li": ("sbuf", [128, L], "int32"), "ci": ("sbuf", [128, L], "int32"),
    "cb": ("sbuf", [128, L], "bfloat16"), "q16": ("sbuf", [128, L], "uint16"), "qf": ("sbuf", [128, L], "float32"),
    "qt": ("sbuf", [128, 12, 32], "float32"), "k1s": ("sbuf", [128, 24, 16], "float32"), "kk": ("sbuf", [128, 24, 16], "float32"),
    "t8": ("sbuf", [128, 24, 8], "float32"), "t4": ("sbuf", [128, 24, 4], "float32"), "t2": ("sbuf", [128, 24, 2], "float32"),
    "ki": ("sbuf", [128, 24], "int32"), "ni": ("sbuf", [128, 24], "int32"), "ii": ("sbuf", [128, 24], "int32"),
    "nl": ("sbuf", [128, 24], "uint16"), "il": ("sbuf", [128, 24], "uint16"), "sl": ("sbuf", [128, 24], "uint16"),
    "ol": ("sbuf", [128, 24], "uint16"), "al": ("sbuf", [128, 24], "uint16"),
    "f1": ("sbuf", [128, 24], "float32"), "f2": ("sbuf", [128, 24], "float32"), "f3": ("sbuf", [128, 24], "float32"),
    "e1": ("sbuf", [128, 24], "float32"), "e2": ("sbuf", [128, 24], "float32"), "e3": ("sbuf", [128, 24], "float32"),
    "g0": ("sbuf", [128, 24], "float32"), "g1": ("sbuf", [128, 24], "float32"), "g2": ("sbuf", [128, 24], "float32"),
    "g3": ("sbuf", [128, 24], "float32"), "g4": ("sbuf", [128, 24], "float32"), "g5": ("sbuf", [128, 24], "float32"),
    "g6": ("sbuf", [128, 24], "float32"), "basev": ("sbuf", [128, 24], "float32"), "ho": ("sbuf", [128, 24], "float32"),
    "x1": ("sbuf", [128, L], "float32"), "xx": ("sbuf", [128, L], "bfloat16"), "xt": ("sbuf", [128, L], "bfloat16"),
    "ng": ("sbuf", [128, L], "bfloat16"), "nd": ("sbuf", [128, L], "bfloat16"), "wv": ("sbuf", [128, L], "bfloat16"),
    "nh": ("sbuf", [128, L], "float16"), "ag": ("sbuf", [128, L], "bfloat16"), "p0": ("sbuf", [128, L], "float32"),
    "ab": ("sbuf", [128, L], "float32"), "th": ("sbuf", [128, L], "bfloat16"), "tn": ("sbuf", [128, L], "bfloat16"),
    "td": ("sbuf", [128, L], "bfloat16"), "pp": ("sbuf", [128, L], "float32"), "st": ("sbuf", [128, L], "float32"),
    "ss": ("sbuf", [128, L], "float16"), "qn": ("sbuf", [128, L], "float32"), "q2": ("sbuf", [128, L], "float32"),
    "ps0": ("psum", [128, 512], "float32"), "ps1": ("psum", [128, 512], "float32"), "ps2": ("psum", [128, 512], "float32"),
    "key0": ("psum", [128, 512], "float32"), "key1": ("psum", [128, 512], "float32"), "cv": ("psum", [128, 512], "float32"),
    "rb": ("psum", [128, 512], "float32"), "k1": ("psum", [128, 12, 2, 16], "float32"),
}
SEMAPHORES = ["qv", "qa", "qt", "qp", "dwk", "dvp", "dqu", "dam", "dpay", "dyv", "dyw", "dyc", "arr0", "arr1", "arr2", "sent"]


def make_queues(g, T):
    ops, last_w, readers = [], {}, {}

    def op(q, fn, r=(), w=(), dma=None, ext=None):
        deps = [(last_w[k], "raw") for k in r if k in last_w]
        for k in w:
            if k in last_w:
                deps.append((last_w[k], "waw"))
            deps += [(o, "war") for o in readers.get(k, ())]
        i = len(ops)
        ops.append({"q": q, "fn": fn, "deps": deps, "dma": dma, "ext": ext, "inc": False})
        for k in w:
            last_w[k] = i
            readers[k] = []
        for k in r:
            readers.setdefault(k, []).append(i)

    def emit():
        engine = {"v": g.vector, "a": g.scalar, "t": g.tensor, "p": g, "s": g.sync}
        sem = {"v": T.sem.qv, "a": T.sem.qa, "t": T.sem.qt, "p": T.sem.qp}
        known = {q: {} for q in engine}
        seq = {q: 0 for q in engine}
        waits = []
        for o in ops:
            o["seq"] = seq[o["q"]]
            if o["ext"] is None:
                seq[o["q"]] += 1
            need = {}
            kn = known[o["q"]]
            for j, kind in o["deps"]:
                d = ops[j]
                if d["ext"] is not None or d["dma"] is not None:
                    name = d["ext"] or d["dma"]
                    if kn.get(name[0], 0) < name[1]:
                        need[name[0]] = (max(need.get(name[0], (0, 0))[0], name[1]), j)
                    continue
                if d["q"] == o["q"] and o["dma"] is None and (kind == "war" or o["q"] == "t"):
                    continue
                if kn.get(d["q"], -1) < d["seq"] and need.get(d["q"], (-1, 0))[0] < d["seq"]:
                    need[d["q"]] = (d["seq"], j)
            for key, (val, j) in need.items():
                for k2, v2 in ops[j]["clock"].items():
                    if k2 != key and kn.get(k2, -1) < v2:
                        kn[k2] = v2
            final = []
            for key, (val, j) in need.items():
                if not any(k2 != key and ops[j2]["clock"].get(key, -1) >= val for k2, (v2, j2) in need.items()):
                    final.append((key, val, j))
                    if key in sem:
                        ops[j]["inc"] = True
                kn[key] = max(kn.get(key, -1), val)
            o["clock"] = dict(kn)
            waits.append(final)
        count = {q: 0 for q in engine}
        for o in ops:
            count[o["q"]] += 1 if o["inc"] else 0
            o["count"] = count[o["q"]]
        for i, o in enumerate(ops):
            if o["ext"] is not None:
                continue
            e = engine[o["q"]]
            for key, val, j in waits[i]:
                e.wait_ge(sem[key] if key in sem else T.sem[key], ops[j]["count"] if key in sem else val)
            ins = o["fn"](e)
            if o["dma"] is not None:
                ins.then_inc(T.sem[o["dma"][0]], 16)
            elif o["inc"]:
                ins.then_inc(sem[o["q"]], 1)
        for q in sem:
            if count[q]:
                g.wait_ge(sem[q], count[q])
    return op, emit


def rank_program(g, core, T, topo):
    rank = T.rank_of(core)
    if rank is None:
        return
    op, emit = make_queues(g, T)
    c_m, c_g, c_p, c_x, c_h0, c_h1, c_ctr, c_sub, c_sgn, c_ini, c_i13, c_n13, c_wn, c_t, c_sg2 = range(15)

    def col(k):
        return T.col[:, k:k + 1]

    def ts(out, in0, s1, s2, o0, o1, r, w):
        op("v", (lambda e: e.tensor_scalar(out, in0, s1, s2, o0, o1)) if o1 else (lambda e: e.tensor_scalar(out, in0, s1, None, o0)), r, w)

    def tt(out, in0, in1, o, r, w):
        op("v", lambda e: e.tensor_tensor(out, in0, in1, o), r, w)

    def tc(out, in_, r, w):
        op("v", lambda e: e.tensor_copy(out, in_), r, w)

    def fill(out, k, w):
        op("v", lambda e: e.memset(out, k), [], w)

    def act(out, in_, f, r, w, bias=0.0, scale=1.0):
        op("a", lambda e: e.activation(out, in_, f, bias=bias, scale=scale), r, w)

    def mm(out, lhs, rhs, start, stop, r, w):
        op("t", lambda e: e.matmul(out, lhs, rhs, start, stop), r, w)

    def iota(out, pattern, base, cm, w):
        op("p", lambda e: e.iota(out, pattern, base, cm, allow_small_or_imprecise_dtypes=True), [], w)

    fill(T.wkz[:], 0, ["wkz"])
    op("s", lambda e: e.dma_start(T.wkz[0::16, :], T.wk[:]), [], ["wkz"], dma=("dwk", 16))
    op("s", lambda e: e.dma_start(T.qw[:, 0:B], T.qu[:]), [], ["qw"], dma=("dqu", 16))
    op("a", lambda e: e.dma_start(T.vw[:, 0:B], T.vp[:]), [], ["vw"], dma=("dvp", 16))
    op("s", lambda e: e.dma_start(T.aw[:, 0:W], T.am[:]), [], ["aw"], dma=("dam", 16))
    for j in range(16):
        op("s", lambda e, j=j: e.dma_start(T.pw[j::16, :], T.pay[:]), ["aw"] if j == 0 else [], ["pw%d" % j], dma=("dpay", 256))

    op("p", lambda e: e.iota(T.pi[:, 0:1], [[1, 1]], 0, 1), [], ["pi0"])
    iota(T.iog[:], [[1, 8], [0, 16]], 0, 0, ["iog"])
    iota(T.io128[:], [[1, 128]], 0, 0, ["io128"])
    iota(T.io16[:], [[1, 16]], 0, 0, ["io16"])
    iota(T.trv[:], [[16, 24]], 2064, 1, ["trv"])
    iota(T.ir[:], [[1, 128], [0, 16]], 0, 0, ["ir"])
    iota(T.hw[:, 0:4096], [[2, 4096]], -4096, 0, ["hw"])
    iota(T.hw[:, 4096:W - 1], [[2, W - 1 - 4096]], -2047, 0, ["hwb"])
    iota(T.hw[:, W - 1:W], [[1, 1]], 5000, 0, ["hwc"])
    for s in range(RO):
        for d in range(NR):
            a0 = PITCH * d + 1
            iota(T["sw%d" % s][:, a0:a0 + CAP], [[0, CAP]], (d * B + B) * 512, 0, ["sw%d_%d" % (s, d)])
    fill(T.vw[:, B:B + 16], 0.0, ["vwp"])
    fill(T.qw[:, B:B + 16], W - 1, ["qwp"])
    fill(T.zb[:], 0.0, ["zb"])
    fill(T.lm[:], 0.0, ["lm0"])
    fill(T.wn[:, 16:32], 0.0, ["wnb"])
    ts(T.pi[:, 1:2], T.pi[:, 0:1], 15, None, A.bitwise_and, None, ["pi0"], ["pi1"])
    ts(T.pi[:, 2:3], T.pi[:, 0:1], 4, None, A.arith_shift_right, None, ["pi0"], ["pi2"])
    ts(T.pi[:, 3:4], T.pi[:, 0:1], 4, 1, A.arith_shift_right, A.bitwise_and, ["pi0"], ["pi3"])
    tc(col(c_p), T.pi[:, 0:1], ["pi0"], ["c_p"])
    tc(col(c_m), T.pi[:, 1:2], ["pi1"], ["c_m"])
    tc(col(c_g), T.pi[:, 2:3], ["pi2"], ["c_g"])
    tc(col(c_h1), T.pi[:, 3:4], ["pi3"], ["c_h1"])
    ts(col(c_h0), col(c_h1), -1.0, 1.0, A.mult, A.add, ["c_h1"], ["c_h0"])
    ts(col(c_x), col(c_h1), -32.0, 16.0, A.mult, A.add, ["c_h1"], ["c_x0"])
    ts(T.bo[:], T.iog[:], col(c_g), None, A.is_equal, None, ["iog", "c_g"], ["bo"])
    tt(col(c_x), col(c_x), col(c_p), A.add, ["c_x0", "c_p"], ["c_x"])
    for k, (pc, hc) in enumerate(((c_p, c_h0), (c_x, c_h0), (c_p, c_h1), (c_x, c_h1))):
        ts(T.dsf[:, k, :], T.io128[:], col(pc), col(hc), A.is_equal, A.mult, ["io128", "c_p", "c_x", "c_h0", "c_h1"], ["dsf%d" % k])
    for k in range(4):
        tc(T.dsb[:, k, :], T.dsf[:, k, :], ["dsf%d" % k], ["dsb%d" % k])
    dsf = ["dsf%d" % k for k in range(4)]
    dsb = ["dsb%d" % k for k in range(4)]
    ts(T.idb[:], T.io128[:], col(c_p), None, A.is_equal, None, ["io128", "c_p"], ["idb"])
    for a in range(16):
        ts(T.lm[:, a, a::16], T.bo[:, 0::16], SC, None, A.mult, None, ["bo", "lm0"], ["lm%d" % (a + 1)])
    ts(col(c_i13), col(c_m), 8192.0, None, A.mult, None, ["c_m"], ["c_i13"])
    ts(col(c_n13), col(c_m), -8192.0, None, A.mult, None, ["c_m"], ["c_n13"])
    ts(col(c_wn), col(c_m), 8192.0, float(W - 1), A.mult, A.add, ["c_m"], ["c_wn"])
    ts(col(c_ctr), col(c_m), -2048.0, -1023.5, A.mult, A.add, ["c_m"], ["c_ctr"])
    ts(col(c_ini), col(c_m), float(PITCH), -1592.0, A.mult, A.add, ["c_m"], ["c_ini"])
    ts(col(c_sgn), col(c_m), 8.0, -2.0, A.is_equal, A.mult, ["c_m"], ["c_sgn0"])
    ts(col(c_t), col(c_m), 8.0, 999.0, A.is_gt, A.mult, ["c_m"], ["c_t"])
    ts(col(c_sub), col(c_m), 8.0, -1.25, A.is_equal, A.mult, ["c_m"], ["c_sub0"])
    ts(T.wc[:, 0:16], T.io16[:], col(c_m), None, A.is_gt, None, ["io16", "c_m"], ["wc0"])
    ts(T.wc[:, 16:32], T.io16[:], col(c_m), -0.5, A.is_equal, A.mult, ["io16", "c_m"], ["wc1"])
    tc(T.bp[:], T.bo[:], ["bo"], ["bp0"])
    ts(T.wn[:, 0:16], T.io16[:], col(c_m), col(c_wn), A.is_equal, A.mult, ["io16", "c_m", "c_wn"], ["wna"])
    ts(col(c_sgn), col(c_sgn), 1.0, None, A.add, None, ["c_sgn0"], ["c_sgn"])
    ts(col(c_sg2), col(c_sgn), -2.0, None, A.mult, None, ["c_sgn"], ["c_sg2"])
    tt(col(c_sub), col(c_sub), col(c_t), A.add, ["c_sub0", "c_t"], ["c_sub1"])
    tt(T.wc[:, 32:48], T.wc[:, 0:16], T.wc[:, 16:32], A.add, ["wc0", "wc1"], ["wc"])
    ts(T.bp[:, 8::16], T.bo[:, 8::16], -1.0, None, A.mult, None, ["bo", "bp0"], ["bp"])
    ts(col(c_sub), col(c_sub), 1.0, None, A.add, None, ["c_sub1"], ["c_sub"])
    for a in range(16):
        ts(T.tm[:, a, :], T.bp[:], T.wc[:, 32 + a:33 + a], None, A.mult, None, ["bp", "wc"], ["tm%d" % a])
    ts(T.rm[:], T.ir[:], col(c_p), None, A.is_equal, None, ["ir", "c_p"], ["rm"])
    tc(T.w16[:], T.wkz[:], ["wkz"], ["w16"])
    tc(T.tt[:], T.wkz[:], ["wkz"], ["tt"])
    op("v", lambda e: e.transpose(T.yy[:], T.tt[:]), ["tt"], ["yy"])
    tc(T.tq[:], T.yy[:, 0::16], ["yy"], ["tq"])

    lms = ["lm%d" % a for a in range(17)]
    tms = ["tm%d" % a for a in range(16)]
    ees = ["ee%d" % c for c in range(24)] + ["ee%dx" % c for c in range(12)]

    def compare(buf, own, key, own_key, h=None):
        for c in range(12 if h == 0 else 24):
            lo = 192 if h == 1 and c < 12 else 16 * c
            hi = 192 if h == 0 else L
            ts(T.ee[:, c, lo - 16 * c:hi - 16 * c], buf[:, lo:hi], own[:, c:c + 1], None, A.is_equal, None,
               [key + "0" if h is not None else key, own_key + "0" if c < 12 and h is not None else own_key] + ([key] if h == 1 else []),
               ["ee%d%s" % (c, "x" if h == 0 else "")])

    def pairs(part=0, parts=1):
        calls = [lambda: mm(T.rb[:, 0:L], T.lm[:, 15, :], T.zb[:], True, False, lms + ["zb"], ["rb"])]
        for c in range(23):
            calls.append(lambda c=c: mm(T.rb[:, 16 * (c + 1):L], T.bp[:], T.ee[:, c, 16:L - 16 * c], False, False,
                                        ["bp", "ee%d" % c] + (["ee%dx" % c] if c < 12 else []), ["rb"]))
        for a in range(16):
            calls.append(lambda a=a: mm(T.rb[:, a:L:16], T.tm[:, a, :], T.ee[:, :, a], False, a == 15, tms + ees, ["rb"]))
        n = len(calls)
        for f in calls[n * part // parts:n * (part + 1) // parts]:
            f()

    def spread(src, key, c0):
        for a in range(16):
            mm(T.cv[:, c0:c0 + 24], T.lm[:, a, :], src[:, a::16], a == 0, a == 15, lms + [key], ["cv"])

    def gather(u):
        act(T.gg[:, 512 * u:512 * (u + 1)], T.aw[:, 0:W].indirect(T.q16[:, 32 * u:32 * (u + 1)]), F.Copy, ["aw", "q16"], ["gg%d" % u])

    def addv(u):
        pk = "ps%d" % (u % 3)
        mm(T[pk][:], T.idb[:], T.gg[:, 512 * u:512 * (u + 1)], True, False, ["idb", "gg%d" % u], [pk])
        mm(T[pk][:], T.xt[:, 128 * (u // 4):128 * (u // 4 + 1)], T.rm[:, 512 * (u % 4):512 * (u % 4 + 1)], False, True, ["xt", "rm"], [pk])

    def sign(u):
        pk = "ps%d" % (u % 3)
        act(T.cc[:, 2 * u:2 * u + 2, :], T[pk][:], F.Sign, [], [pk, "cc%d" % u, "ccb%d" % u], bias=0.5)

    def score(q):
        kb, off = "key%d" % (q // 3), 64 * (q % 3)
        for a in range(16):
            mm(T[kb][:, off:off + 64], T.lm[:, a, :], T.cc[:, 4 * q:4 * q + 4, 16 * a:16 * a + 16], a == 0, a == 15,
               lms + ["cc%d" % (2 * q), "cc%d" % (2 * q + 1), "ccb%d" % (2 * q), "ccb%d" % (2 * q + 1)], [kb])

    def best(h):
        kb, hs, n = "key%d" % h, slice(12 * h, 12 * h + 12), "%d" % h
        tt(T.kk[:, hs, :], T[kb][:, 0:192], T.k1s[:, hs, :], A.add, ["k1s"], [kb, "kk" + n])
        tt(T.t8[:, hs, :], T.kk[:, hs, 0:8], T.kk[:, hs, 8:16], A.max, ["kk" + n], ["t8" + n])
        tt(T.t4[:, hs, :], T.t8[:, hs, 0:4], T.t8[:, hs, 4:8], A.max, ["t8" + n], ["t4" + n])
        tt(T.t2[:, hs, :], T.t4[:, hs, 0:2], T.t4[:, hs, 2:4], A.max, ["t4" + n], ["t2" + n])
        tt(T.ki[:, hs], T.t2[:, hs, 0], T.t2[:, hs, 1], A.max, ["t2" + n], ["ki" + n])

    def own_units(c0, c1):
        for c in range(c0, c1):
            tt(T.cc[:, c, :], T.aw[:, 0:W].indirect(T.q16[:, 16 * c:16 * c + 16]), T.vr[:, 256 * c:256 * c + 256], A.is_ge,
               ["aw", "q16"] + ["vr%d" % i for i in range(16)], ["cc%d" % (c // 2) if c % 2 else "ccb%d" % (c // 2)])

    def lines(h):
        hs, n, ls = slice(12 * h, 12 * h + 12), "%d" % h, slice(192 * h, 192 * h + 192)
        ts(T.ni[:, hs], T.ki[:, hs], 8191, None, A.bitwise_and, None, ["ki" + n], ["ni" + n])
        tc(T.nl[:, hs], T.ni[:, hs], ["ni" + n], ["nl" + n])
        ts(T.f1[:, hs], T.ni[:, hs], 4096.0, -6143.0, A.is_ge, A.mult, ["ni" + n], ["f1" + n])
        ts(T.f2[:, hs], T.ni[:, hs], 2.0, -4096.0, A.mult, A.add, ["ni" + n], ["f2" + n])
        tc(T.nh[:, ls], T.hw[:].indirect(T.nl[:, hs]), ["hw", "hwb", "hwc", "nl" + n], ["nh" + n if h == 0 else "nh"])
        tt(T.f3[:, hs], T.f1[:, hs], T.basev[:, hs], A.add, ["f1" + n, "basev"], ["f3" + n])
        tt(T.ho[:, hs], T.f3[:, hs], T.f2[:, hs], A.add, ["f3" + n, "f2" + n], ["ho" + n if h == 0 else "ho"])

    def send(s, to_buf):
        def fn(e):
            tr = []
            nth = [0, 0]
            for d in range(1, NR):
                to = (rank + d) % NR
                dst = T.cores[to]
                rid, pid, _ = topo.addr(dst)
                near = int(topo.die(dst) == topo.die(core))
                k = 4 * nth[near] + near
                nth[near] += 1
                m = sum(1 << x for x in topo.engines(core, dst)[k:k + 3:2])
                tr.append(RemoteDMATransfer(dst_ids=[DstId(rid=rid, pnc=pid)], dma_engine_mask=m, remote_sem=T.sem["arr%d" % s],
                                            srcs=[T["sw%d" % s][:, PITCH * to + 1:PITCH * to + 1 + CAP]],
                                            dsts=[T[to_buf][:, CAP * rank:CAP * (rank + 1)]]))
            return e.remote_dma_fused(tr, local_sem=T.sem.sent)
        return fn

    for s in range(RO):
        lk = "land%d" % s
        lks = [lk, lk + "o"]
        if s:
            land = T[lk]
            op("v", lambda e, land=land: e.transpose(T.tt[:], land[:]), lks, ["tt"])
            ts(T.tqi[:], T.tt[:, 0::16], 1.0 / 512, -float(B * rank), A.mult, A.add, ["tt"], ["tqi"])
            tc(T.tq[:], T.tqi[:], ["tqi"], ["tq"])
            act(T.yy[:], land[:], F.Identity, lks, ["yy"], bias=BIG - B * rank, scale=1.0 / 512)
            tc(T.li[:], land[:], lks, ["li"])
        else:
            mm(T.rb[:, 0:L], T.bo[:], T.w16[:], True, True, ["bo", "w16"], ["rb"])
        for cc in range(2):
            for k in range(2):
                mm(T.cv[:, cc:24:2], T.dsb[:, 2 * cc + k, :], T.tq[:, (cc ^ k)::2], k == 0, k == 1, dsb + ["tq"], ["cv"])
        tc(T.bl[:], T.cv[:, 0:24], [], ["cv", "bl"])
        act(T.bf[:], T.cv[:, 0:24], F.Copy, [], ["cv", "bf"])
        tc(T.q16[:], T.qw[:, 0:B + 16].indirect(T.bl[:]), ["qw", "qwp", "bl"], ["q16"])
        ts(T.qf[:], T.q16[:], col(c_i13), None, A.add, None, ["q16", "c_i13"], ["qf"])
        op("v", lambda e: e.transpose(T.qt[:], T.qf[:]), ["qf"], ["qt"])
        for cc in range(2):
            for j in range(2):
                gx = 16 * (cc ^ j)
                mm(T.k1[:, :, cc, :], T.dsf[:, 2 * cc + j, :], T.qt[:, :, gx:gx + 16], j == 0, j == 1, dsf + ["qt"], ["k1"])
        if s:
            ts(T.ci[:], T.li[:], 511, None, A.bitwise_and, None, ["li"], ["ci"])
            tt(T.x1[:], T.vw[:, 0:B + 16].indirect(T.bl[:]), T.ci[:], A.subtract, ["vw", "vwp", "bl", "ci"], ["x1"])
            ts(T.xx[:], T.x1[:], -255.0, None, A.max, None, ["x1"], ["xx"])
        else:
            act(T.xx[:], T.vw[:, 0:B + 16].indirect(T.bl[:]), F.Copy, ["vw", "vwp", "bl"], ["xx"])
        k0 = NA // 4
        for k in range(k0, 3):
            mm(T.cv[:, 128 * (k + 1):128 * (k + 2)], T.xx[:, 128 * k:128 * (k + 1)], T.idb[:], True, True, ["xx", "idb"], ["cv"])
        units = list(range(NA, 12))
        gather(units[0])
        gather(units[1])
        act(T.xt[:, 128 * k0:L], T.cv[:, 128 * (k0 + 1):512], F.Copy, [], ["cv", "xt"])
        if s:
            ts(T.b16[:], T.yy[:], -BIG, None, A.add, None, ["yy"], ["b16"])
        else:
            tc(T.b16[:], T.rb[:, 0:L], [], ["rb", "b16"])
        ts(T.ng[:], T.xx[:], 0.0, 64.0, A.is_lt, A.add, ["xx"], ["ng"])
        compare(T.b16, T.bf, "b16", "bf")
        for i in range(16):
            ts(T.vr[:, i:512 * NA:16], T.xx[:, 0:32 * NA], -1.0, None, A.mult, None, ["xx"], ["vr%d" % i])
        addv(units[0])
        for k in range(2, len(units) + 2):
            if k < len(units):
                gather(units[k])
            sign(units[k - 2])
            if k - 1 < len(units):
                addv(units[k - 1])
            own_units(*C_OWN.get(k, (0, 0)))
            if K_PAIRS <= k < K_PAIRS + N_PAIRS:
                pairs(k - K_PAIRS, N_PAIRS)
            if k == K_ND:
                ts(T.rb[:, 0:L], T.rb[:, 0:L], col(c_sgn), 0.0, A.mult, A.is_lt, ["c_sgn"], ["rb"])
                tt(T.wv[:], T.ng[:], T.rb[:, 0:L], A.mult, ["ng"], ["rb", "wv"])
            if k == K_VAL:
                spread(T.wv, "wv", 48)
            if k == K_BASE:
                ts(T.basev[:], T.cv[:, 48:72], 1024.5 * SC, 20000.0, A.is_lt, A.mult, [], ["cv", "basev"])
                ts(T.e1[:], T.cv[:, 48:72], 0.5 * SC, None, A.is_lt, None, [], ["cv", "e1"])
                tt(T.e2[:], T.e1[:], T.trv[:], A.mult, ["e1", "trv"], ["e2"])
                tt(T.e3[:], T.e2[:], T.bf[:], A.max, ["e2", "bf"], ["e3"])
                tc(T.ol[:], T.e3[:], ["e3"], ["ol"])
            if k == K_SCORE:
                for q in range(NA // 2):
                    score(q)
                tc(T.k1s[:], T.k1[:], [], ["k1", "k1s"])
            if units[k - 2] % 2:
                score(units[k - 2] // 2)
            if k == K_BEST:
                best(0)
                lines(0)
                compare(T.nh, T.ho, "nh", "ho", 0)
        act(T.k1[:], T.xx[:], F.Relu, ["xx"], ["k1"], scale=-1.0)
        best(1)
        lines(1)
        act(T.p0[:], T.pw[:, 0:W].indirect(T.nl[:]), F.Copy, ["pw15", "nl0", "nl1"], ["p0"], scale=512.0)
        act(T.ag[:], T.aw[:, 0:W].indirect(T.nl[:]), F.Copy, ["aw", "nl0", "nl1"], ["ag"])
        act(T.ab[:], T.p0[:], F.Abs, ["p0", "c_ctr"], ["ab"], bias=col(c_ctr), scale=1.0 / 512)
        compare(T.nh, T.ho, "nh", "ho", 1)
        pairs()
        ts(T.th[:], T.ab[:], 1024.0, col(c_sub), A.is_lt, A.subtract, ["ab", "c_sub"], ["th"])
        tt(T.k1[:], T.ag[:], T.k1[:], A.min, ["ag"], ["k1"])
        tt(T.ps2[:, 0:L], T.rb[:, 0:L], T.th[:], A.is_lt, ["th"], ["rb", "ps2"])
        op("v", lambda e: e.tensor_tensor_scan(T.st[:], T.ps2[:, 0:L], T.zb[:], col(c_ini), A.add, A.add), ["zb", "c_ini"], ["ps2", "st"])
        tt(T.ss[:], T.st[:], T.ps2[:, 0:L], A.mult, ["st"], ["ps2", "ss"])
        spread(T.ss, "ss", 24)
        tt(T.pp[:], T.p0[:], T.k1[:], A.add, ["p0"], ["k1", "pp"])
        ts(T.sl[:], T.cv[:, 24:48], 1.0 / SC, 1592.0, A.mult, A.add, [], ["cv", "sl"])
        swk = ["sw%d_%d" % (s, d) for d in range(NR)]
        tc(T["sw%d" % s][:].indirect(T.sl[:]), T.pp[:], ["sl", "pp"], swk)
        nk = "land%d" % (s + 1)
        op("p", send(s, nk), swk, [])
        op("p", None, [], [nk], ext=("arr%d" % s, 2 * (NR - 1)))
        if s < RO - 1:
            act(T.g0[:], T.cv[:, 24:48], F.Sign, [], ["cv", "g0"], bias=-1600.0, scale=1.0 / SC)
            act(T.g2[:], T.cv[:, 24:48], F.Copy, [], ["cv", "g2"], bias=4535.0, scale=1.0 / SC)
            act(T.tn[:], T.k1[:], F.Copy, [], ["k1", "tn"], scale=-1.0)
            act(T.g1[:], T.g0[:], F.Relu, ["g0"], ["g1"])
            act(T.g4[:], T.g0[:], F.Relu, ["g0"], ["g4"], scale=16.0)
        act(T.nd[:], T.rb[:, 0:L], F.Relu, ["c_sg2"], ["rb", "nd"], scale=col(c_sg2))
        a0 = PITCH * rank + 1
        act(T[nk][:, CAP * rank:CAP * (rank + 1)], T["sw%d" % s][:, a0:a0 + CAP], F.Copy, swk, [nk + "o"])
        if s < RO - 1:
            ts(T.ii[:], T.ki[:], 13, 15, A.arith_shift_right, A.bitwise_and, ["ki0", "ki1"], ["ii"])
            tt(T.g3[:], T.g1[:], T.g2[:], A.mult, ["g1", "g2"], ["g3"])
            tt(T.g5[:], T.g4[:], T.ii[:], A.add, ["g4", "ii"], ["g5"])
            tc(T.il[:], T.g5[:], ["g5"], ["il"])
            tt(T.qn[:], T.wn[:].indirect(T.il[:]), T.qf[:], A.max, ["wna", "wnb", "il", "qf"], ["qn"])
            act(T.q2[:], T.qn[:], F.Identity, ["qn", "c_n13"], ["q2"], bias=col(c_n13))
        tt(T.td[:], T.nd[:], T.k1[:], A.mult, ["nd"], ["k1", "td"])
        if s < RO - 1:
            tt(T.g6[:], T.g3[:], T.ni[:], A.max, ["g3", "ni0", "ni1"], ["g6"])
            tc(T.qw[:].indirect(T.ol[:]), T.q2[:], ["ol", "q2"], ["qw", "qwp"])
            tc(T.al[:], T.g6[:], ["g6"], ["al"])
        tt(T.vw[:].indirect(T.ol[:]), T.xx[:], T.td[:], A.add, ["ol", "xx", "td"], ["vw", "vwp"])
        if s < RO - 1:
            tt(T.aw[:].indirect(T.al[:]), T.ag[:], T.tn[:], A.add, ["al", "ag", "tn"], ["aw"])
        else:
            op("s", lambda e: e.dma_start(T.yv[:], T.vw[:, 0:B]), ["vw"], ["yv"], dma=("dyv", 16))

    lk = "land%d" % RO
    lks = [lk, lk + "o"]
    act(T.yy[:], T[lk][:], F.Identity, lks, ["yy"], bias=BIG - B * rank, scale=1.0 / 512)
    act(T.x1[:], T.yy[:], F.Identity, ["yy"], ["x1"], bias=-BIG)
    op("a", lambda e: e.dma_start(T.yw[:], T.x1[0::16, :]), ["x1"], ["yw"], dma=("dyw", 16))
    tc(T.li[:], T[lk][:], lks, ["li"])
    ts(T.ci[:], T.li[:], 511, None, A.bitwise_and, None, ["li"], ["ci"])
    tc(T.cb[:], T.ci[:], ["ci"], ["cb"])
    op("s", lambda e: e.dma_start(T.yc[:], T.cb[:]), ["cb"], ["yc"], dma=("dyc", 16))
    emit()
    g.wait_ge(T.sem.sent, 2 * (NR - 1) * RO)
    for n in ("dyv", "dyw", "dyc", "dwk", "dvp", "dqu", "dam"):
        g.wait_ge(T.sem[n], 16)
    g.wait_ge(T.sem.dpay, 256)
